import numpy as np
import ml_dtypes


def mxq(x, axis, fmt="e4m3"):
    dtype, down = {"e4m3": (ml_dtypes.float8_e4m3fn, 7), "e5m2": (ml_dtypes.float8_e5m2, 14)}[fmt]
    v = np.moveaxis(np.asarray(x, np.float32).astype(ml_dtypes.bfloat16).astype(np.float64), axis, -1)
    blocks = v.reshape(v.shape[:-1] + (-1, 32))
    amax = np.abs(blocks).max(-1, keepdims=True)
    byte = np.maximum(np.where(amax > 0, np.frexp(amax)[1] - 1 + 127, 0) - down, 1)
    scale = np.exp2(byte - 127.0)
    codes = (blocks / scale).astype(np.float32).astype(dtype).astype(np.float64)
    return np.moveaxis((codes * scale).reshape(v.shape), -1, axis)


WIDE = False


def mx_kscale(k):
    if not WIDE:
        return np.ones(k)
    levels = np.array([30, -30])
    if k % 512:
        return np.exp2(np.random.permutation(np.resize(levels, k // 32))).repeat(32)
    a = np.empty((k // 512, 16))
    for p in range(k // 512):
        a[p, :8] = np.random.permutation(np.resize(levels, 8))
        for g in range(8):
            far = levels[np.abs(levels - a[p, g]) >= 10]
            a[p, g + 8] = far[np.random.randint(len(far))]
    return np.exp2(a.ravel()).repeat(32)


def f64(x):
    return np.asarray(x).astype(np.float64)


E2M1 = np.array([0.0, 0.5, 1.0, 1.5, 2.0, 3.0, 4.0, 6.0, -0.0, -0.5, -1.0, -1.5, -2.0, -3.0, -4.0, -6.0])


def pack_weight(w, fmt):
    k, n = w.shape
    w = f64(np.asarray(w, np.float32).astype(ml_dtypes.bfloat16)).reshape(k // 32, 32, n)
    amax = np.abs(w).max(1)
    if fmt == "e4m3":
        byte = np.frexp(amax)[1] - 1 + 127 - 7
    else:
        mant, ex = np.frexp(amax / 6.0)
        byte = np.where(mant > 0.5, ex, ex - 1) + 127
    byte = np.clip(np.where(amax > 0, byte, 1), 1, 254)
    scaled = (w * np.exp2(127.0 - byte)[:, None, :]).reshape(k, n).astype(np.float32)
    by_word = np.ascontiguousarray(scaled.reshape(k // 512, 128, 4, n).transpose(0, 1, 3, 2))
    if fmt == "e4m3":
        words = by_word.astype(ml_dtypes.float8_e4m3fn).view(np.uint8)
    else:
        c = by_word.astype(ml_dtypes.float4_e2m1fn).view(np.uint8) & 0xF
        words = (c[..., 0::2] | (c[..., 1::2] << 4)).reshape(k // 512, 128, 2 * n)
    return np.ascontiguousarray(words), np.ascontiguousarray(byte.astype(np.uint8).reshape(k // 512, 16, n))


def unpack_weight(words, scales, fmt):
    g, _, n = scales.shape
    words = np.ascontiguousarray(words).reshape(g, 128, n, -1)
    if fmt == "e4m3":
        vals = words.view(ml_dtypes.float8_e4m3fn).astype(np.float64)
    else:
        nib = np.empty((g, 128, n, 4), np.uint8)
        nib[..., 0::2] = words & 0xF
        nib[..., 1::2] = words >> 4
        vals = E2M1[nib]
    vals = vals * np.repeat(np.exp2(scales.astype(np.float64) - 127.0), 8, axis=1)[..., None]
    return vals.transpose(0, 1, 3, 2).reshape(g * 512, n)


K, L, M, N = 1024, 1024, 1024, 1024


def setup_inputs():
    n = np.random.standard_normal
    s = mx_kscale(K)[:, None]
    u = mx_kscale(L)[:, None]
    am = n((K, M)) / s
    bm = n((L, N)) / np.sqrt(L) / u
    b4 = pack_weight(bm, "e2m1")
    rest = bm - unpack_weight(*b4, "e2m1")
    p_a8 = pack_weight(am[:512], "e4m3")
    p_a4 = pack_weight(am[512:], "e2m1")
    p_b8 = pack_weight(rest, "e4m3")
    return {
        "g": (n((K, L)) / np.sqrt(K) * s * u.T).astype(np.float32),
        "a8_words": p_a8[0],
        "a8_scales": p_a8[1],
        "a4_words": p_a4[0],
        "a4_scales": p_a4[1],
        "b4_words": b4[0],
        "b4_scales": b4[1],
        "b8_words": p_b8[0],
        "b8_scales": p_b8[1],
        "prm": (0.1 * n((M, N))).astype(np.float32),
    }


def reference(g, a8_words, a8_scales, a4_words, a4_scales, b4_words, b4_scales, b8_words, b8_scales, prm):
    g_ = mxq(f64(g), 0, "e5m2")
    a8_ = unpack_weight(a8_words, a8_scales, "e4m3")
    a4_ = unpack_weight(a4_words, a4_scales, "e2m1")
    h = g_[:512].T @ a8_ + g_[512:].T @ a4_
    h_ = mxq(h, 0, "e5m2")
    b4_ = unpack_weight(b4_words, b4_scales, "e2m1")
    b8_ = unpack_weight(b8_words, b8_scales, "e4m3")
    y = h_.T @ b4_ + h_.T @ b8_
    return f64(prm) - 0.0625 * y

@@ -1,0 +1,266 @@
+from contextlib import ExitStack
+
+import concourse.mybir as mybir
+
+K, L, M, N = 1024, 1024, 1024, 1024
+FLOPS = 2 * K * L * M + 2 * 2 * L * M * N
+
+F32 = mybir.dt.float32
+BF16 = mybir.dt.bfloat16
+I32 = mybir.dt.int32
+U8 = mybir.dt.uint8
+E4M3 = mybir.dt.float8_e4m3fn_x4
+E5M2 = mybir.dt.float8_e5m2_x4
+E2M1 = mybir.dt.float4_e2m1fn_x4
+MULT = mybir.AluOpType.mult
+ADD = mybir.AluOpType.add
+
+P = 128
+PACK = 4
+PASS = P * PACK
+BANK = 512
+STEP = -0.0625
+HALF = P // 2
+
+
+def tile_mix_kfac_mix_res_sgd_kernel(
+    tc, g, a8_words, a8_scales, a4_words, a4_scales, b4_words, b4_scales, b8_words, b8_scales, prm, out
+):
+    nc = tc.nc
+    with ExitStack() as ctx:
+        sb = ctx.enter_context(tc.tile_pool(name="sb", bufs=1))
+        psum = ctx.enter_context(tc.psum_pool(name="psum", bufs=1))
+        ctx.enter_context(tc.manual_schedule())
+
+        def tile(name, shape, dtype):
+            return sb.tile(shape, dtype, name=name, align_bytes=64)
+
+        banks = [psum.tile([P, BANK], F32, name="bank%d" % i) for i in range(8)]
+
+        a8_plane = tile("a8_plane", [P, 1, M], U8)
+        a4_plane = tile("a4_plane", [P, 1, M], U8)
+        b4_plane = tile("b4_plane", [P, 2, N], U8)
+        b8_plane = tile("b8_plane", [P, 2, N], U8)
+        for plane in (a4_plane, a8_plane, b4_plane, b8_plane):
+            nc.vector.memset(plane[:].bitcast(I32), 0)
+
+        def load_scales(plane, scales):
+            for r in range(4):
+                nc.sync.dma_start(
+                    out=plane[r:P:32, :, :].bitcast(I32),
+                    in_=scales[:, r:16:4, :].rearrange("a q n -> q a n").bitcast(I32),
+                )
+
+        g_raw = {}
+
+        def load_g(kh, lh, half):
+            raw = tile("g_raw%d%d%d" % (kh, lh, half), [P, PACK, PASS // 2], F32)
+            l0 = lh * PASS + half * (PASS // 2)
+            nc.sync.dma_start(
+                out=raw[:],
+                in_=g[kh * PASS : (kh + 1) * PASS, l0 : l0 + PASS // 2].rearrange("(p t) w -> p t w", t=PACK),
+            )
+            g_raw[kh, lh, half] = raw
+
+        def load_fp8(name, words):
+            dst = tile(name, [P, N], I32)
+            nc.sync.dma_start(out=dst[:], in_=words.rearrange("p n t -> p (n t)").bitcast(I32))
+            return dst
+
+        def load_fp4(name, words):
+            dst = tile(name, [P, 2 * N], U8)
+            nc.sync.dma_start(out=dst[:].bitcast(I32), in_=words.bitcast(I32))
+            return dst
+
+        load_g(1, 0, 0)
+        load_g(1, 0, 1)
+        a4 = load_fp4("a4", a4_words[0])
+        load_scales(a4_plane, a4_scales)
+        load_g(0, 0, 0)
+        load_g(0, 0, 1)
+        a8 = load_fp8("a8", a8_words[0])
+        load_scales(a8_plane, a8_scales)
+        for kh in (1, 0):
+            load_g(kh, 1, 0)
+            load_g(kh, 1, 1)
+        b4 = [load_fp4("b4_0", b4_words[0])]
+        load_scales(b4_plane, b4_scales)
+        b8 = [load_fp8("b8_0", b8_words[0])]
+        b4.append(load_fp4("b4_1", b4_words[1]))
+        load_scales(b8_plane, b8_scales)
+        b8.append(load_fp8("b8_1", b8_words[1]))
+        prm_sb = []
+        for mt in range(M // P):
+            rows = tile("prm%d" % mt, [P, N], F32)
+            nc.sync.dma_start(out=rows[:], in_=prm[mt * P : (mt + 1) * P, :])
+            prm_sb.append(rows)
+
+        g_bf = {(kh, lh): tile("g_bf%d%d" % (kh, lh), [P, PACK, P, PACK], BF16) for kh in range(2) for lh in range(2)}
+        g_codes, g_scale = {}, {}
+
+        def copy(engine, dst, src):
+            if engine is nc.scalar:
+                nc.scalar.copy(out=dst, in_=src)
+            else:
+                nc.vector.tensor_copy(out=dst, in_=src)
+
+        def cast_g(engine, kh, lh, half, c0=0, c1=HALF):
+            dst = g_bf[kh, lh][:, :, half * HALF + c0 : half * HALF + c1, :].rearrange("p j c t -> p c j t")
+            src = g_raw[kh, lh, half][:, :, PACK * c0 : PACK * c1].rearrange("p t (c j) -> p c j t", j=PACK)
+            copy(engine, dst, src)
+
+        def cast_g_shared(kh, lh, half):
+            cast_g(nc.scalar, kh, lh, half, 0, 20)
+            cast_g(nc.vector, kh, lh, half, 20, HALF)
+
+        def quantize_g(kh, lh):
+            for j in range(PACK):
+                codes = tile("g_codes%d%d%d" % (kh, lh, j), [P, P], I32)
+                scale = tile("g_scale%d%d%d" % (kh, lh, j), [P, P], U8)
+                nc.vector.quantize_mx(
+                    out=codes[:].bitcast(E5M2),
+                    scales=scale[:],
+                    in_=g_bf[kh, lh][:, j, :, :].rearrange("p c t -> p (c t)"),
+                )
+                g_codes[kh, lh, j], g_scale[kh, lh, j] = codes, scale
+
+        def first_product(kh, lh, mh):
+            cols = slice(mh * BANK, (mh + 1) * BANK)
+            if kh == 0:
+                rhs, rhs_scale = a8[:, cols].bitcast(E4M3), a8_plane[:, 0, cols]
+            else:
+                rhs, rhs_scale = a4[:, 2 * cols.start : 2 * cols.stop].bitcast(E2M1), a4_plane[:, 0, cols]
+            for j in range(PACK):
+                nc.tensor.matmul_mx(
+                    out=banks[PACK * mh + j][:],
+                    lhsT=g_codes[kh, lh, j][:].bitcast(E5M2),
+                    lhsT_scale=g_scale[kh, lh, j][:],
+                    rhs=rhs,
+                    rhs_scale=rhs_scale,
+                    start=(kh == 1),
+                    stop=(kh == 0),
+                )
+
+        h_rows = {(lh, mh): tile("h_rows%d%d" % (lh, mh), [P, PACK, BANK], BF16) for lh in range(2) for mh in range(2)}
+        h_bf, h_codes, h_scale = {}, {}, {}
+
+        def drain_h(engine, lh, mh, j):
+            copy(engine, h_rows[lh, mh][:, j, :], banks[PACK * mh + j][:])
+
+        def interleave_h(lh, mt):
+            dst = tile("h_bf%d%d" % (lh, mt), [P, P, PACK], BF16)
+            c0 = (mt % 4) * P
+            src = h_rows[lh, mt // 4][:, :, c0 : c0 + P]
+            nc.vector.tensor_copy(
+                out=dst[:].rearrange("p (c i) j -> p c j i", i=4),
+                in_=src.rearrange("p j (c i) -> p c j i", i=4),
+            )
+            h_bf[lh, mt] = dst
+
+        def quantize_h(lh, mt):
+            codes = tile("h_codes%d%d" % (lh, mt), [P, P], I32)
+            scale = tile("h_scale%d%d" % (lh, mt), [P, P], U8)
+            nc.vector.quantize_mx(
+                out=codes[:].bitcast(E5M2), scales=scale[:], in_=h_bf[lh, mt][:].rearrange("p c j -> p (c j)")
+            )
+            h_codes[lh, mt], h_scale[lh, mt] = codes, scale
+
+        def pack_h(lh, mts):
+            for mt in mts:
+                interleave_h(lh, mt)
+            for mt in mts:
+                quantize_h(lh, mt)
+
+        def y_bank(mt, nh):
+            return banks[(2 * mt + nh) % 8]
+
+        def second_product(mt, nh, lh):
+            cols = slice(nh * BANK, (nh + 1) * BANK)
+            operands = (
+                (b4[lh][:, 2 * cols.start : 2 * cols.stop].bitcast(E2M1), b4_plane[:, lh, cols]),
+                (b8[lh][:, cols].bitcast(E4M3), b8_plane[:, lh, cols]),
+            )
+            for tier, (rhs, rhs_scale) in enumerate(operands):
+                nc.tensor.matmul_mx(
+                    out=y_bank(mt, nh)[:],
+                    lhsT=h_codes[lh, mt][:].bitcast(E5M2),
+                    lhsT_scale=h_scale[lh, mt][:],
+                    rhs=rhs,
+                    rhs_scale=rhs_scale,
+                    start=(lh == 0 and tier == 0),
+                    stop=(lh == 1 and tier == 1),
+                )
+
+        res = [tile("res%d" % mt, [P, N], F32) for mt in range(M // P)]
+
+        def update(mt, nh, c0=0, c1=BANK):
+            cols = slice(nh * BANK + c0, nh * BANK + c1)
+            nc.vector.scalar_tensor_tensor(
+                out=res[mt][:, cols],
+                in0=y_bank(mt, nh)[:, c0:c1],
+                scalar=STEP,
+                in1=prm_sb[mt][:, cols],
+                op0=MULT,
+                op1=ADD,
+            )
+
+        def store(mt, c0, c1):
+            nc.sync.dma_start(out=out[mt * P : (mt + 1) * P, c0:c1], in_=res[mt][:, c0:c1])
+
+        cast_g(nc.vector, 1, 0, 0)
+        cast_g_shared(1, 0, 1)
+        quantize_g(1, 0)
+        first_product(1, 0, 0)
+        first_product(1, 0, 1)
+        cast_g(nc.scalar, 0, 0, 0)
+        cast_g_shared(0, 0, 1)
+        quantize_g(0, 0)
+        first_product(0, 0, 0)
+        first_product(0, 0, 1)
+        cast_g(nc.vector, 1, 1, 0)
+        drain_h(nc.scalar, 0, 0, 0)
+        drain_h(nc.vector, 0, 0, 1)
+        drain_h(nc.scalar, 0, 0, 2)
+        drain_h(nc.scalar, 0, 0, 3)
+        for j in range(PACK):
+            drain_h(nc.scalar, 0, 1, j)
+        cast_g(nc.vector, 1, 1, 1)
+        quantize_g(1, 1)
+        first_product(1, 1, 0)
+        first_product(1, 1, 1)
+        cast_g(nc.vector, 0, 1, 0)
+        pack_h(0, (0, 1))
+        cast_g_shared(0, 1, 1)
+        quantize_g(0, 1)
+        first_product(0, 1, 0)
+        first_product(0, 1, 1)
+        drain_h(nc.scalar, 1, 0, 0)
+        drain_h(nc.vector, 1, 0, 1)
+        drain_h(nc.scalar, 1, 0, 2)
+        drain_h(nc.vector, 1, 0, 3)
+        for j in range(PACK):
+            drain_h(nc.scalar, 1, 1, j)
+        pack_h(1, (0, 1))
+        pack_h(0, (2, 3))
+        pack_h(1, (2, 3))
+
+        for mt in range(M // P):
+            if mt == 0:
+                order = [(0, 0), (1, 0), (0, 1), (1, 1)]
+            else:
+                order = [(0, 0), (0, 1), (1, 0), (1, 1)]
+            for nh, lh in order:
+                second_product(mt, nh, lh)
+            update(mt, 0)
+            if mt == M // P - 1:
+                store(mt, 0, BANK)
+                update(mt, 1, 0, BANK // 2)
+                store(mt, BANK, BANK + BANK // 2)
+                update(mt, 1, BANK // 2, BANK)
+                store(mt, BANK + BANK // 2, N)
+            else:
+                update(mt, 1)
+                store(mt, 0, N)
+            if mt < 2:
+                pack_h(0, (4 + 2 * mt, 5 + 2 * mt))
+                pack_h(1, (4 + 2 * mt, 5 + 2 * mt))

@@ -53,14 +53,16 @@ def tile_mix_kfac_mix_res_sgd_kernel(
 
         g_raw = {}
 
-        def load_g(kh, lh, half):
-            raw = tile("g_raw%d%d%d" % (kh, lh, half), [P, PACK, PASS // 2], F32)
-            l0 = lh * PASS + half * (PASS // 2)
+        def load_g(kh, lh, c0, c1):
+            raw = tile("g_raw%d%d_%d" % (kh, lh, c0), [P, PACK, PACK * (c1 - c0)], F32)
+            l0 = lh * PASS
             nc.sync.dma_start(
                 out=raw[:],
-                in_=g[kh * PASS : (kh + 1) * PASS, l0 : l0 + PASS // 2].rearrange("(p t) w -> p t w", t=PACK),
+                in_=g[kh * PASS : (kh + 1) * PASS, l0 + PACK * c0 : l0 + PACK * c1].rearrange(
+                    "(p t) w -> p t w", t=PACK
+                ),
             )
-            g_raw[kh, lh, half] = raw
+            g_raw[kh, lh, c0] = raw
 
         def load_fp8(name, words):
             dst = tile(name, [P, N], I32)
@@ -72,27 +74,27 @@ def tile_mix_kfac_mix_res_sgd_kernel(
             nc.sync.dma_start(out=dst[:].bitcast(I32), in_=words.bitcast(I32))
             return dst
 
-        load_g(1, 0, 0)
-        load_g(1, 0, 1)
+        load_g(1, 0, 0, P)
         a4 = load_fp4("a4", a4_words[0])
         load_scales(a4_plane, a4_scales)
-        load_g(0, 0, 0)
-        load_g(0, 0, 1)
+        load_g(0, 0, 0, P)
         a8 = load_fp8("a8", a8_words[0])
         load_scales(a8_plane, a8_scales)
         for kh in (1, 0):
-            load_g(kh, 1, 0)
-            load_g(kh, 1, 1)
-        b4 = [load_fp4("b4_0", b4_words[0])]
+            load_g(kh, 1, 0, HALF)
+            load_g(kh, 1, HALF, P)
+        b4 = tile("b4", [P, 2, 2 * N], U8)
+        nc.sync.dma_start(out=b4[:].bitcast(I32), in_=b4_words.rearrange("a p w -> p a w").bitcast(I32))
         load_scales(b4_plane, b4_scales)
         b8 = [load_fp8("b8_0", b8_words[0])]
-        b4.append(load_fp4("b4_1", b4_words[1]))
         load_scales(b8_plane, b8_scales)
         b8.append(load_fp8("b8_1", b8_words[1]))
         prm_sb = []
-        for mt in range(M // P):
-            rows = tile("prm%d" % mt, [P, N], F32)
-            nc.sync.dma_start(out=rows[:], in_=prm[mt * P : (mt + 1) * P, :])
+        for pair in range(M // (2 * P)):
+            rows = tile("prm%d" % pair, [P, 2, N], F32)
+            nc.sync.dma_start(
+                out=rows[:], in_=prm[2 * pair * P : 2 * (pair + 1) * P, :].rearrange("(e p) n -> p e n", p=P)
+            )
             prm_sb.append(rows)
 
         g_bf = {(kh, lh): tile("g_bf%d%d" % (kh, lh), [P, PACK, P, PACK], BF16) for kh in range(2) for lh in range(2)}
@@ -104,14 +106,14 @@ def tile_mix_kfac_mix_res_sgd_kernel(
             else:
                 nc.vector.tensor_copy(out=dst, in_=src)
 
-        def cast_g(engine, kh, lh, half, c0=0, c1=HALF):
-            dst = g_bf[kh, lh][:, :, half * HALF + c0 : half * HALF + c1, :].rearrange("p j c t -> p c j t")
-            src = g_raw[kh, lh, half][:, :, PACK * c0 : PACK * c1].rearrange("p t (c j) -> p c j t", j=PACK)
-            copy(engine, dst, src)
+        def cast_g(engine, kh, lh, first, c0, c1):
+            dst = g_bf[kh, lh][:, :, c0:c1, :].rearrange("p j c t -> p c j t")
+            src = g_raw[kh, lh, first][:, :, PACK * (c0 - first) : PACK * (c1 - first)]
+            copy(engine, dst, src.rearrange("p t (c j) -> p c j t", j=PACK))
 
-        def cast_g_shared(kh, lh, half):
-            cast_g(nc.scalar, kh, lh, half, 0, 20)
-            cast_g(nc.vector, kh, lh, half, 20, HALF)
+        def cast_g_shared(kh, lh, c0, split, c1):
+            cast_g(nc.scalar, kh, lh, c0, c0, split)
+            cast_g(nc.vector, kh, lh, c0, split, c1)
 
         def quantize_g(kh, lh):
             for j in range(PACK):
@@ -147,112 +149,122 @@ def tile_mix_kfac_mix_res_sgd_kernel(
         def drain_h(engine, lh, mh, j):
             copy(engine, h_rows[lh, mh][:, j, :], banks[PACK * mh + j][:])
 
-        def interleave_h(lh, mt):
-            dst = tile("h_bf%d%d" % (lh, mt), [P, P, PACK], BF16)
-            c0 = (mt % 4) * P
-            src = h_rows[lh, mt // 4][:, :, c0 : c0 + P]
-            nc.vector.tensor_copy(
-                out=dst[:].rearrange("p (c i) j -> p c j i", i=4),
-                in_=src.rearrange("p j (c i) -> p c j i", i=4),
-            )
-            h_bf[lh, mt] = dst
+        def interleave_h(engine, lh, mt0, count):
+            dst = tile("h_bf%d%d" % (lh, mt0), [P, count * P, PACK], BF16)
+            c0 = (mt0 % 4) * P
+            src = h_rows[lh, mt0 // 4][:, :, c0 : c0 + count * P]
+            copy(engine, dst[:].rearrange("p (c i) j -> p c j i", i=4), src.rearrange("p j (c i) -> p c j i", i=4))
+            h_bf[lh, mt0] = dst
 
-        def quantize_h(lh, mt):
-            codes = tile("h_codes%d%d" % (lh, mt), [P, P], I32)
-            scale = tile("h_scale%d%d" % (lh, mt), [P, P], U8)
+        def quantize_h(lh, mt0, count):
+            codes = tile("h_codes%d%d" % (lh, mt0), [P, count * P], I32)
+            scale = tile("h_scale%d%d" % (lh, mt0), [P, count * P], U8)
             nc.vector.quantize_mx(
-                out=codes[:].bitcast(E5M2), scales=scale[:], in_=h_bf[lh, mt][:].rearrange("p c j -> p (c j)")
+                out=codes[:].bitcast(E5M2), scales=scale[:], in_=h_bf[lh, mt0][:].rearrange("p c j -> p (c j)")
             )
-            h_codes[lh, mt], h_scale[lh, mt] = codes, scale
-
-        def pack_h(lh, mts):
-            for mt in mts:
-                interleave_h(lh, mt)
-            for mt in mts:
-                quantize_h(lh, mt)
+            for i in range(count):
+                h_codes[lh, mt0 + i] = codes[:, i * P : (i + 1) * P]
+                h_scale[lh, mt0 + i] = scale[:, i * P : (i + 1) * P]
 
         def y_bank(mt, nh):
             return banks[(2 * mt + nh) % 8]
 
-        def second_product(mt, nh, lh):
+        def second_product(mt, nh, lh, tier):
             cols = slice(nh * BANK, (nh + 1) * BANK)
-            operands = (
-                (b4[lh][:, 2 * cols.start : 2 * cols.stop].bitcast(E2M1), b4_plane[:, lh, cols]),
-                (b8[lh][:, cols].bitcast(E4M3), b8_plane[:, lh, cols]),
+            if tier == 0:
+                rhs, rhs_scale = b4[:, lh, 2 * cols.start : 2 * cols.stop].bitcast(E2M1), b4_plane[:, lh, cols]
+            else:
+                rhs, rhs_scale = b8[lh][:, cols].bitcast(E4M3), b8_plane[:, lh, cols]
+            nc.tensor.matmul_mx(
+                out=y_bank(mt, nh)[:],
+                lhsT=h_codes[lh, mt].bitcast(E5M2),
+                lhsT_scale=h_scale[lh, mt],
+                rhs=rhs,
+                rhs_scale=rhs_scale,
+                start=(lh == 0 and tier == 0),
+                stop=(lh == 1 and tier == 1),
             )
-            for tier, (rhs, rhs_scale) in enumerate(operands):
-                nc.tensor.matmul_mx(
-                    out=y_bank(mt, nh)[:],
-                    lhsT=h_codes[lh, mt][:].bitcast(E5M2),
-                    lhsT_scale=h_scale[lh, mt][:],
-                    rhs=rhs,
-                    rhs_scale=rhs_scale,
-                    start=(lh == 0 and tier == 0),
-                    stop=(lh == 1 and tier == 1),
-                )
 
-        res = [tile("res%d" % mt, [P, N], F32) for mt in range(M // P)]
+        res = [tile("res%d" % pair, [P, 2, N], F32) for pair in range(M // (2 * P))]
 
         def update(mt, nh, c0=0, c1=BANK):
             cols = slice(nh * BANK + c0, nh * BANK + c1)
             nc.vector.scalar_tensor_tensor(
-                out=res[mt][:, cols],
+                out=res[mt // 2][:, mt % 2, cols],
                 in0=y_bank(mt, nh)[:, c0:c1],
                 scalar=STEP,
-                in1=prm_sb[mt][:, cols],
+                in1=prm_sb[mt // 2][:, mt % 2, cols],
                 op0=MULT,
                 op1=ADD,
             )
 
         def store(mt, c0, c1):
-            nc.sync.dma_start(out=out[mt * P : (mt + 1) * P, c0:c1], in_=res[mt][:, c0:c1])
+            nc.sync.dma_start(out=out[mt * P : (mt + 1) * P, c0:c1], in_=res[mt // 2][:, mt % 2, c0:c1])
 
-        cast_g(nc.vector, 1, 0, 0)
-        cast_g_shared(1, 0, 1)
-        quantize_g(1, 0)
-        first_product(1, 0, 0)
-        first_product(1, 0, 1)
-        cast_g(nc.scalar, 0, 0, 0)
-        cast_g_shared(0, 0, 1)
-        quantize_g(0, 0)
-        first_product(0, 0, 0)
-        first_product(0, 0, 1)
-        cast_g(nc.vector, 1, 1, 0)
+        def store_pair(pair):
+            nc.sync.dma_start(
+                out=out[2 * pair * P : 2 * (pair + 1) * P, :].rearrange("(e p) n -> p e n", p=P), in_=res[pair][:]
+            )
+
+        for kh in (1, 0):
+            cast_g_shared(kh, 0, 0, 44, P)
+            quantize_g(kh, 0)
+            first_product(kh, 0, 0)
+            first_product(kh, 0, 1)
         drain_h(nc.scalar, 0, 0, 0)
         drain_h(nc.vector, 0, 0, 1)
+        cast_g(nc.vector, 1, 1, 0, 0, HALF)
         drain_h(nc.scalar, 0, 0, 2)
-        drain_h(nc.scalar, 0, 0, 3)
+        drain_h(nc.vector, 0, 0, 3)
         for j in range(PACK):
             drain_h(nc.scalar, 0, 1, j)
-        cast_g(nc.vector, 1, 1, 1)
+        cast_g(nc.vector, 1, 1, HALF, HALF, P)
         quantize_g(1, 1)
         first_product(1, 1, 0)
         first_product(1, 1, 1)
-        cast_g(nc.vector, 0, 1, 0)
-        pack_h(0, (0, 1))
-        cast_g_shared(0, 1, 1)
+        cast_g(nc.vector, 0, 1, 0, 0, HALF)
+        cast_g_shared(0, 1, HALF, HALF + 20, P)
         quantize_g(0, 1)
         first_product(0, 1, 0)
         first_product(0, 1, 1)
+        interleave_h(nc.vector, 0, 0, 2)
         drain_h(nc.scalar, 1, 0, 0)
         drain_h(nc.vector, 1, 0, 1)
+        quantize_h(0, 0, 2)
         drain_h(nc.scalar, 1, 0, 2)
-        drain_h(nc.vector, 1, 0, 3)
+        drain_h(nc.scalar, 1, 0, 3)
         for j in range(PACK):
             drain_h(nc.scalar, 1, 1, j)
-        pack_h(1, (0, 1))
-        pack_h(0, (2, 3))
-        pack_h(1, (2, 3))
+        interleave_h(nc.vector, 0, 2, 2)
+        interleave_h(nc.vector, 1, 0, 2)
+        quantize_h(0, 2, 2)
+        quantize_h(1, 0, 2)
+        interleave_h(nc.vector, 1, 2, 2)
+        for mt0 in (4, 6):
+            for lh in range(2):
+                interleave_h(nc.scalar, lh, mt0, 2)
 
-        for mt in range(M // P):
-            if mt == 0:
-                order = [(0, 0), (1, 0), (0, 1), (1, 1)]
-            else:
-                order = [(0, 0), (0, 1), (1, 0), (1, 1)]
-            for nh, lh in order:
-                second_product(mt, nh, lh)
+        for lh in range(2):
+            for tier in range(2):
+                for mt in range(2):
+                    for nh in range(2):
+                        second_product(mt, nh, lh, tier)
+        quantize_h(1, 2, 2)
+        for mt in range(2):
             update(mt, 0)
-            if mt == M // P - 1:
+            update(mt, 1)
+        store_pair(0)
+        last = M // P - 1
+        for mt in range(2, M // P):
+            for nh in range(2):
+                for lh in range(2):
+                    for tier in range(2):
+                        second_product(mt, nh, lh, tier)
+            if mt in (2, 3):
+                for lh in range(2):
+                    quantize_h(lh, 2 * mt, 2)
+            update(mt, 0)
+            if mt == last:
                 store(mt, 0, BANK)
                 update(mt, 1, 0, BANK // 2)
                 store(mt, BANK, BANK + BANK // 2)
@@ -260,7 +272,7 @@ def tile_mix_kfac_mix_res_sgd_kernel(
                 store(mt, BANK + BANK // 2, N)
             else:
                 update(mt, 1)
-                store(mt, 0, N)
-            if mt < 2:
-                pack_h(0, (4 + 2 * mt, 5 + 2 * mt))
-                pack_h(1, (4 + 2 * mt, 5 + 2 * mt))
+                if mt == last - 1:
+                    store(mt, 0, N)
+                elif mt % 2 == 1:
+                    store_pair(mt // 2)

@@ -74,7 +74,8 @@ def tile_mix_kfac_mix_res_sgd_kernel(
             nc.sync.dma_start(out=dst[:].bitcast(I32), in_=words.bitcast(I32))
             return dst
 
-        load_g(1, 0, 0, P)
+        load_g(1, 0, 0, HALF)
+        load_g(1, 0, HALF, P)
         a4 = load_fp4("a4", a4_words[0])
         load_scales(a4_plane, a4_scales)
         load_g(0, 0, 0, P)
@@ -206,36 +207,42 @@ def tile_mix_kfac_mix_res_sgd_kernel(
                 out=out[2 * pair * P : 2 * (pair + 1) * P, :].rearrange("(e p) n -> p e n", p=P), in_=res[pair][:]
             )
 
-        for kh in (1, 0):
-            cast_g_shared(kh, 0, 0, 44, P)
-            quantize_g(kh, 0)
-            first_product(kh, 0, 0)
-            first_product(kh, 0, 1)
+        cast_g(nc.vector, 1, 0, 0, 0, HALF)
+        cast_g_shared(1, 0, HALF, HALF + 20, P)
+        quantize_g(1, 0)
+        first_product(1, 0, 0)
+        first_product(1, 0, 1)
+        cast_g_shared(0, 0, 0, 44, P)
+        quantize_g(0, 0)
+        first_product(0, 0, 0)
+        first_product(0, 0, 1)
         drain_h(nc.scalar, 0, 0, 0)
         drain_h(nc.vector, 0, 0, 1)
-        cast_g(nc.vector, 1, 1, 0, 0, HALF)
         drain_h(nc.scalar, 0, 0, 2)
-        drain_h(nc.vector, 0, 0, 3)
+        cast_g(nc.vector, 1, 1, 0, 0, HALF)
+        cast_g_shared(1, 1, HALF, HALF + 20, P)
+        drain_h(nc.scalar, 0, 0, 3)
         for j in range(PACK):
             drain_h(nc.scalar, 0, 1, j)
-        cast_g(nc.vector, 1, 1, HALF, HALF, P)
         quantize_g(1, 1)
         first_product(1, 1, 0)
         first_product(1, 1, 1)
         cast_g(nc.vector, 0, 1, 0, 0, HALF)
-        cast_g_shared(0, 1, HALF, HALF + 20, P)
+        cast_g(nc.vector, 0, 1, HALF, HALF, P)
+        interleave_h(nc.vector, 0, 0, 1)
         quantize_g(0, 1)
         first_product(0, 1, 0)
         first_product(0, 1, 1)
-        interleave_h(nc.vector, 0, 0, 2)
+        quantize_h(0, 0, 1)
         drain_h(nc.scalar, 1, 0, 0)
         drain_h(nc.vector, 1, 0, 1)
-        quantize_h(0, 0, 2)
         drain_h(nc.scalar, 1, 0, 2)
         drain_h(nc.scalar, 1, 0, 3)
         for j in range(PACK):
             drain_h(nc.scalar, 1, 1, j)
+        interleave_h(nc.vector, 0, 1, 1)
         interleave_h(nc.vector, 0, 2, 2)
+        quantize_h(0, 1, 1)
         interleave_h(nc.vector, 1, 0, 2)
         quantize_h(0, 2, 2)
         quantize_h(1, 0, 2)

@@ -108,9 +108,9 @@ def tile_mix_kfac_mix_res_sgd_kernel(
                 nc.vector.tensor_copy(out=dst, in_=src)
 
         def cast_g(engine, kh, lh, first, c0, c1):
-            dst = g_bf[kh, lh][:, :, c0:c1, :].rearrange("p j c t -> p c j t")
+            dst = g_bf[kh, lh][:, :, c0:c1, :].rearrange("p j c t -> p c t j")
             src = g_raw[kh, lh, first][:, :, PACK * (c0 - first) : PACK * (c1 - first)]
-            copy(engine, dst, src.rearrange("p t (c j) -> p c j t", j=PACK))
+            copy(engine, dst, src.rearrange("p t (c j) -> p c t j", j=PACK))
 
         def cast_g_shared(kh, lh, c0, split, c1):
             cast_g(nc.scalar, kh, lh, c0, c0, split)

@@ -20,7 +20,7 @@ PACK = 4
 PASS = P * PACK
 BANK = 512
 STEP = -0.0625
-HALF = P // 2
+SHARE = 48
 
 
 def tile_mix_kfac_mix_res_sgd_kernel(
@@ -74,16 +74,14 @@ def tile_mix_kfac_mix_res_sgd_kernel(
             nc.sync.dma_start(out=dst[:].bitcast(I32), in_=words.bitcast(I32))
             return dst
 
-        load_g(1, 0, 0, HALF)
-        load_g(1, 0, HALF, P)
+        load_g(1, 0, 0, P)
         a4 = load_fp4("a4", a4_words[0])
         load_scales(a4_plane, a4_scales)
         load_g(0, 0, 0, P)
         a8 = load_fp8("a8", a8_words[0])
         load_scales(a8_plane, a8_scales)
         for kh in (1, 0):
-            load_g(kh, 1, 0, HALF)
-            load_g(kh, 1, HALF, P)
+            load_g(kh, 1, 0, P)
         b4 = tile("b4", [P, 2, 2 * N], U8)
         nc.sync.dma_start(out=b4[:].bitcast(I32), in_=b4_words.rearrange("a p w -> p a w").bitcast(I32))
         load_scales(b4_plane, b4_scales)
@@ -207,46 +205,43 @@ def tile_mix_kfac_mix_res_sgd_kernel(
                 out=out[2 * pair * P : 2 * (pair + 1) * P, :].rearrange("(e p) n -> p e n", p=P), in_=res[pair][:]
             )
 
-        cast_g(nc.vector, 1, 0, 0, 0, HALF)
-        cast_g_shared(1, 0, HALF, HALF + 20, P)
+        cast_g_shared(1, 0, 0, SHARE, P)
         quantize_g(1, 0)
         first_product(1, 0, 0)
         first_product(1, 0, 1)
-        cast_g_shared(0, 0, 0, 44, P)
+        cast_g_shared(0, 0, 0, SHARE, P)
         quantize_g(0, 0)
         first_product(0, 0, 0)
         first_product(0, 0, 1)
         drain_h(nc.scalar, 0, 0, 0)
         drain_h(nc.vector, 0, 0, 1)
         drain_h(nc.scalar, 0, 0, 2)
-        cast_g(nc.vector, 1, 1, 0, 0, HALF)
-        cast_g_shared(1, 1, HALF, HALF + 20, P)
-        drain_h(nc.scalar, 0, 0, 3)
-        for j in range(PACK):
-            drain_h(nc.scalar, 0, 1, j)
+        drain_h(nc.vector, 0, 0, 3)
+        drain_h(nc.scalar, 0, 1, 0)
+        cast_g_shared(1, 1, 0, SHARE, P)
+        drain_h(nc.scalar, 0, 1, 2)
+        drain_h(nc.scalar, 0, 1, 3)
         quantize_g(1, 1)
+        drain_h(nc.vector, 0, 1, 1)
         first_product(1, 1, 0)
         first_product(1, 1, 1)
-        cast_g(nc.vector, 0, 1, 0, 0, HALF)
-        cast_g(nc.vector, 0, 1, HALF, HALF, P)
-        interleave_h(nc.vector, 0, 0, 1)
+        cast_g_shared(0, 1, 0, SHARE, P)
         quantize_g(0, 1)
         first_product(0, 1, 0)
         first_product(0, 1, 1)
-        quantize_h(0, 0, 1)
+        interleave_h(nc.vector, 0, 0, 2)
         drain_h(nc.scalar, 1, 0, 0)
         drain_h(nc.vector, 1, 0, 1)
         drain_h(nc.scalar, 1, 0, 2)
-        drain_h(nc.scalar, 1, 0, 3)
+        quantize_h(0, 0, 2)
+        drain_h(nc.vector, 1, 0, 3)
         for j in range(PACK):
             drain_h(nc.scalar, 1, 1, j)
-        interleave_h(nc.vector, 0, 1, 1)
-        interleave_h(nc.vector, 0, 2, 2)
-        quantize_h(0, 1, 1)
         interleave_h(nc.vector, 1, 0, 2)
-        quantize_h(0, 2, 2)
+        interleave_h(nc.vector, 0, 2, 2)
         quantize_h(1, 0, 2)
         interleave_h(nc.vector, 1, 2, 2)
+        quantize_h(0, 2, 2)
         for mt0 in (4, 6):
             for lh in range(2):
                 interleave_h(nc.scalar, lh, mt0, 2)

@@ -20,7 +20,8 @@ PACK = 4
 PASS = P * PACK
 BANK = 512
 STEP = -0.0625
-SHARE = 48
+HALF = P // 2
+WARM = 7
 
 
 def tile_mix_kfac_mix_res_sgd_kernel(
@@ -41,7 +42,18 @@ def tile_mix_kfac_mix_res_sgd_kernel(
         a4_plane = tile("a4_plane", [P, 1, M], U8)
         b4_plane = tile("b4_plane", [P, 2, N], U8)
         b8_plane = tile("b8_plane", [P, 2, N], U8)
-        for plane in (a4_plane, a8_plane, b4_plane, b8_plane):
+        zeros = tile("zeros", [P, 2 * BANK], BF16)
+        warm_codes = tile("warm_codes", [P, BANK], I32)
+        warm_scale = tile("warm_scale", [P, BANK], U8)
+        still_codes = tile("still_codes", [P, P], I32)
+        still_scale = tile("still_scale", [P, P], U8)
+        nc.vector.memset(zeros[:].bitcast(I32), 0)
+        nc.vector.memset(a4_plane[:].bitcast(I32), 0)
+        for c0 in (0, BANK // 2):
+            cols = slice(c0, c0 + BANK // 2)
+            nc.vector.quantize_mx(out=warm_codes[:, cols].bitcast(E4M3), scales=warm_scale[:, cols], in_=zeros[:])
+        nc.vector.quantize_mx(out=still_codes[:].bitcast(E5M2), scales=still_scale[:], in_=zeros[:, 0:BANK])
+        for plane in (a8_plane, b4_plane, b8_plane):
             nc.vector.memset(plane[:].bitcast(I32), 0)
 
         def load_scales(plane, scales):
@@ -81,7 +93,8 @@ def tile_mix_kfac_mix_res_sgd_kernel(
         a8 = load_fp8("a8", a8_words[0])
         load_scales(a8_plane, a8_scales)
         for kh in (1, 0):
-            load_g(kh, 1, 0, P)
+            load_g(kh, 1, 0, HALF)
+            load_g(kh, 1, HALF, P)
         b4 = tile("b4", [P, 2, 2 * N], U8)
         nc.sync.dma_start(out=b4[:].bitcast(I32), in_=b4_words.rearrange("a p w -> p a w").bitcast(I32))
         load_scales(b4_plane, b4_scales)
@@ -92,7 +105,7 @@ def tile_mix_kfac_mix_res_sgd_kernel(
         for pair in range(M // (2 * P)):
             rows = tile("prm%d" % pair, [P, 2, N], F32)
             nc.sync.dma_start(
-                out=rows[:], in_=prm[2 * pair * P : 2 * (pair + 1) * P, :].rearrange("(e p) n -> p e n", p=P)
+                out=rows[:], in_=prm[2 * pair * P : 2 * (pair + 1) * P, :].rearrange("(p e) n -> p e n", e=2)
             )
             prm_sb.append(rows)
 
@@ -105,14 +118,15 @@ def tile_mix_kfac_mix_res_sgd_kernel(
             else:
                 nc.vector.tensor_copy(out=dst, in_=src)
 
-        def cast_g(engine, kh, lh, first, c0, c1):
-            dst = g_bf[kh, lh][:, :, c0:c1, :].rearrange("p j c t -> p c t j")
+        def cast_g(engine, kh, lh, first, c0, c1, j0=0, j1=PACK):
+            dst = g_bf[kh, lh][:, j0:j1, c0:c1, :].rearrange("p j c t -> p c t j")
             src = g_raw[kh, lh, first][:, :, PACK * (c0 - first) : PACK * (c1 - first)]
-            copy(engine, dst, src.rearrange("p t (c j) -> p c t j", j=PACK))
+            copy(engine, dst, src.rearrange("p t (c j) -> p c t j", j=PACK)[:, :, :, j0:j1])
 
         def cast_g_shared(kh, lh, c0, split, c1):
-            cast_g(nc.scalar, kh, lh, c0, c0, split)
-            cast_g(nc.vector, kh, lh, c0, split, c1)
+            cast_g(nc.scalar, kh, lh, c0, c0, split, 2, PACK)
+            cast_g(nc.vector, kh, lh, c0, c0, c1, 0, 2)
+            cast_g(nc.vector, kh, lh, c0, split, c1, 2, PACK)
 
         def quantize_g(kh, lh):
             for j in range(PACK):
@@ -152,7 +166,11 @@ def tile_mix_kfac_mix_res_sgd_kernel(
             dst = tile("h_bf%d%d" % (lh, mt0), [P, count * P, PACK], BF16)
             c0 = (mt0 % 4) * P
             src = h_rows[lh, mt0 // 4][:, :, c0 : c0 + count * P]
-            copy(engine, dst[:].rearrange("p (c i) j -> p c j i", i=4), src.rearrange("p j (c i) -> p c j i", i=4))
+            copy(
+                engine,
+                dst[:].rearrange("p (e c q) j -> p c j q e", e=2, q=2),
+                src.rearrange("p j (c q e) -> p c j q e", e=2, q=2),
+            )
             h_bf[lh, mt0] = dst
 
         def quantize_h(lh, mt0, count):
@@ -168,7 +186,7 @@ def tile_mix_kfac_mix_res_sgd_kernel(
         def y_bank(mt, nh):
             return banks[(2 * mt + nh) % 8]
 
-        def second_product(mt, nh, lh, tier):
+        def second_product(mt, nh, lh, tier, start, stop):
             cols = slice(nh * BANK, (nh + 1) * BANK)
             if tier == 0:
                 rhs, rhs_scale = b4[:, lh, 2 * cols.start : 2 * cols.stop].bitcast(E2M1), b4_plane[:, lh, cols]
@@ -180,8 +198,8 @@ def tile_mix_kfac_mix_res_sgd_kernel(
                 lhsT_scale=h_scale[lh, mt],
                 rhs=rhs,
                 rhs_scale=rhs_scale,
-                start=(lh == 0 and tier == 0),
-                stop=(lh == 1 and tier == 1),
+                start=start,
+                stop=stop,
             )
 
         res = [tile("res%d" % pair, [P, 2, N], F32) for pair in range(M // (2 * P))]
@@ -198,34 +216,47 @@ def tile_mix_kfac_mix_res_sgd_kernel(
             )
 
         def store(mt, c0, c1):
-            nc.sync.dma_start(out=out[mt * P : (mt + 1) * P, c0:c1], in_=res[mt // 2][:, mt % 2, c0:c1])
+            rows = out[2 * (mt // 2) * P : 2 * (mt // 2 + 1) * P, :].rearrange("(p e) n -> p e n", e=2)
+            nc.sync.dma_start(out=rows[:, mt % 2, c0:c1], in_=res[mt // 2][:, mt % 2, c0:c1])
 
         def store_pair(pair):
             nc.sync.dma_start(
-                out=out[2 * pair * P : 2 * (pair + 1) * P, :].rearrange("(e p) n -> p e n", p=P), in_=res[pair][:]
+                out=out[2 * pair * P : 2 * (pair + 1) * P, :].rearrange("(p e) n -> p e n", e=2), in_=res[pair][:]
             )
 
-        cast_g_shared(1, 0, 0, SHARE, P)
+        for i in range(WARM):
+            nc.tensor.matmul_mx(
+                out=banks[7][:],
+                lhsT=still_codes[:].bitcast(E5M2),
+                lhsT_scale=still_scale[:],
+                rhs=warm_codes[:].bitcast(E4M3),
+                rhs_scale=warm_scale[:],
+                start=True,
+                stop=True,
+            )
+
+        cast_g_shared(1, 0, 0, 88, P)
         quantize_g(1, 0)
         first_product(1, 0, 0)
         first_product(1, 0, 1)
-        cast_g_shared(0, 0, 0, SHARE, P)
+        cast_g_shared(0, 0, 0, 88, P)
         quantize_g(0, 0)
         first_product(0, 0, 0)
         first_product(0, 0, 1)
         drain_h(nc.scalar, 0, 0, 0)
         drain_h(nc.vector, 0, 0, 1)
         drain_h(nc.scalar, 0, 0, 2)
-        drain_h(nc.vector, 0, 0, 3)
-        drain_h(nc.scalar, 0, 1, 0)
-        cast_g_shared(1, 1, 0, SHARE, P)
-        drain_h(nc.scalar, 0, 1, 2)
-        drain_h(nc.scalar, 0, 1, 3)
+        cast_g(nc.vector, 1, 1, 0, 0, HALF)
+        drain_h(nc.scalar, 0, 0, 3)
+        cast_g(nc.vector, 1, 1, HALF, HALF, P, 0, 2)
+        cast_g(nc.vector, 1, 1, HALF, HALF, P, 2, PACK)
+        for j in range(PACK):
+            drain_h(nc.scalar, 0, 1, j)
         quantize_g(1, 1)
-        drain_h(nc.vector, 0, 1, 1)
         first_product(1, 1, 0)
         first_product(1, 1, 1)
-        cast_g_shared(0, 1, 0, SHARE, P)
+        cast_g(nc.vector, 0, 1, 0, 0, HALF)
+        cast_g_shared(0, 1, HALF, HALF + 24, P)
         quantize_g(0, 1)
         first_product(0, 1, 0)
         first_product(0, 1, 1)
@@ -234,7 +265,7 @@ def tile_mix_kfac_mix_res_sgd_kernel(
         drain_h(nc.vector, 1, 0, 1)
         drain_h(nc.scalar, 1, 0, 2)
         quantize_h(0, 0, 2)
-        drain_h(nc.vector, 1, 0, 3)
+        drain_h(nc.scalar, 1, 0, 3)
         for j in range(PACK):
             drain_h(nc.scalar, 1, 1, j)
         interleave_h(nc.vector, 1, 0, 2)
@@ -250,7 +281,7 @@ def tile_mix_kfac_mix_res_sgd_kernel(
             for tier in range(2):
                 for mt in range(2):
                     for nh in range(2):
-                        second_product(mt, nh, lh, tier)
+                        second_product(mt, nh, lh, tier, lh == 0 and tier == 0, lh == 1 and tier == 1)
         quantize_h(1, 2, 2)
         for mt in range(2):
             update(mt, 0)
@@ -258,10 +289,10 @@ def tile_mix_kfac_mix_res_sgd_kernel(
         store_pair(0)
         last = M // P - 1
         for mt in range(2, M // P):
+            there = [(0, 0), (0, 1), (1, 1), (1, 0)]
             for nh in range(2):
-                for lh in range(2):
-                    for tier in range(2):
-                        second_product(mt, nh, lh, tier)
+                for i, (lh, tier) in enumerate(there if nh == 0 else there[::-1]):
+                    second_product(mt, nh, lh, tier, i == 0, i == 3)
             if mt in (2, 3):
                 for lh in range(2):
                     quantize_h(lh, 2 * mt, 2)

@@ -128,8 +128,8 @@ def tile_mix_kfac_mix_res_sgd_kernel(
             cast_g(nc.vector, kh, lh, c0, c0, c1, 0, 2)
             cast_g(nc.vector, kh, lh, c0, split, c1, 2, PACK)
 
-        def quantize_g(kh, lh):
-            for j in range(PACK):
+        def quantize_g(kh, lh, j0=0, j1=PACK):
+            for j in range(j0, j1):
                 codes = tile("g_codes%d%d%d" % (kh, lh, j), [P, P], I32)
                 scale = tile("g_scale%d%d%d" % (kh, lh, j), [P, P], U8)
                 nc.vector.quantize_mx(
@@ -139,13 +139,13 @@ def tile_mix_kfac_mix_res_sgd_kernel(
                 )
                 g_codes[kh, lh, j], g_scale[kh, lh, j] = codes, scale
 
-        def first_product(kh, lh, mh):
+        def first_product(kh, lh, mh, j0=0, j1=PACK):
             cols = slice(mh * BANK, (mh + 1) * BANK)
             if kh == 0:
                 rhs, rhs_scale = a8[:, cols].bitcast(E4M3), a8_plane[:, 0, cols]
             else:
                 rhs, rhs_scale = a4[:, 2 * cols.start : 2 * cols.stop].bitcast(E2M1), a4_plane[:, 0, cols]
-            for j in range(PACK):
+            for j in range(j0, j1):
                 nc.tensor.matmul_mx(
                     out=banks[PACK * mh + j][:],
                     lhsT=g_codes[kh, lh, j][:].bitcast(E5M2),
@@ -249,23 +249,26 @@ def tile_mix_kfac_mix_res_sgd_kernel(
         cast_g(nc.vector, 1, 1, 0, 0, HALF)
         drain_h(nc.scalar, 0, 0, 3)
         cast_g(nc.vector, 1, 1, HALF, HALF, P, 0, 2)
-        cast_g(nc.vector, 1, 1, HALF, HALF, P, 2, PACK)
+        cast_g(nc.vector, 1, 1, HALF, HALF, HALF + 32, 2, PACK)
+        quantize_g(1, 1, 0, 2)
+        cast_g(nc.vector, 1, 1, HALF, HALF + 32, P, 2, PACK)
         for j in range(PACK):
             drain_h(nc.scalar, 0, 1, j)
-        quantize_g(1, 1)
-        first_product(1, 1, 0)
-        first_product(1, 1, 1)
+        quantize_g(1, 1, 2, PACK)
+        first_product(1, 1, 0, 0, 2)
+        first_product(1, 1, 1, 0, 1)
+        first_product(1, 1, 0, 2, PACK)
+        first_product(1, 1, 1, 1, PACK)
         cast_g(nc.vector, 0, 1, 0, 0, HALF)
         cast_g_shared(0, 1, HALF, HALF + 24, P)
         quantize_g(0, 1)
         first_product(0, 1, 0)
         first_product(0, 1, 1)
         interleave_h(nc.vector, 0, 0, 2)
-        drain_h(nc.scalar, 1, 0, 0)
-        drain_h(nc.vector, 1, 0, 1)
-        drain_h(nc.scalar, 1, 0, 2)
         quantize_h(0, 0, 2)
-        drain_h(nc.scalar, 1, 0, 3)
+        for j in range(3):
+            drain_h(nc.scalar, 1, 0, j)
+        drain_h(nc.vector, 1, 0, 3)
         for j in range(PACK):
             drain_h(nc.scalar, 1, 1, j)
         interleave_h(nc.vector, 1, 0, 2)
@@ -297,8 +300,9 @@ def tile_mix_kfac_mix_res_sgd_kernel(
                 for lh in range(2):
                     quantize_h(lh, 2 * mt, 2)
             update(mt, 0)
-            if mt == last:
+            if mt >= last - 1:
                 store(mt, 0, BANK)
+            if mt == last:
                 update(mt, 1, 0, BANK // 2)
                 store(mt, BANK, BANK + BANK // 2)
                 update(mt, 1, BANK // 2, BANK)
@@ -306,6 +310,8 @@ def tile_mix_kfac_mix_res_sgd_kernel(
             else:
                 update(mt, 1)
                 if mt == last - 1:
+                    store(mt, BANK, N)
+                elif mt >= 4:
                     store(mt, 0, N)
                 elif mt % 2 == 1:
                     store_pair(mt // 2)

@@ -34,7 +34,7 @@ def tile_mix_kfac_mix_res_sgd_kernel(
         ctx.enter_context(tc.manual_schedule())
 
         def tile(name, shape, dtype):
-            return sb.tile(shape, dtype, name=name, align_bytes=64)
+            return sb.tile(shape, dtype, name=name, align_bytes=256)
 
         banks = [psum.tile([P, BANK], F32, name="bank%d" % i) for i in range(8)]
 

@@ -174,14 +174,16 @@ def tile_mix_kfac_mix_res_sgd_kernel(
             h_bf[lh, mt0] = dst
 
         def quantize_h(lh, mt0, count):
-            codes = tile("h_codes%d%d" % (lh, mt0), [P, count * P], I32)
-            scale = tile("h_scale%d%d" % (lh, mt0), [P, count * P], U8)
-            nc.vector.quantize_mx(
-                out=codes[:].bitcast(E5M2), scales=scale[:], in_=h_bf[lh, mt0][:].rearrange("p c j -> p (c j)")
-            )
             for i in range(count):
-                h_codes[lh, mt0 + i] = codes[:, i * P : (i + 1) * P]
-                h_scale[lh, mt0 + i] = scale[:, i * P : (i + 1) * P]
+                codes = tile("h_codes%d%d" % (lh, mt0 + i), [P, P], I32)
+                scale = tile("h_scale%d%d" % (lh, mt0 + i), [P, P], U8)
+                nc.vector.quantize_mx(
+                    out=codes[:].bitcast(E5M2),
+                    scales=scale[:],
+                    in_=h_bf[lh, mt0][:, i * P : (i + 1) * P, :].rearrange("p c j -> p (c j)"),
+                )
+                h_codes[lh, mt0 + i] = codes[:]
+                h_scale[lh, mt0 + i] = scale[:]
 
         def y_bank(mt, nh):
             return banks[(2 * mt + nh) % 8]

@@ -21,7 +21,6 @@ PASS = P * PACK
 BANK = 512
 STEP = -0.0625
 HALF = P // 2
-WARM = 7
 
 
 def tile_mix_kfac_mix_res_sgd_kernel(
@@ -42,18 +41,7 @@ def tile_mix_kfac_mix_res_sgd_kernel(
         a4_plane = tile("a4_plane", [P, 1, M], U8)
         b4_plane = tile("b4_plane", [P, 2, N], U8)
         b8_plane = tile("b8_plane", [P, 2, N], U8)
-        zeros = tile("zeros", [P, 2 * BANK], BF16)
-        warm_codes = tile("warm_codes", [P, BANK], I32)
-        warm_scale = tile("warm_scale", [P, BANK], U8)
-        still_codes = tile("still_codes", [P, P], I32)
-        still_scale = tile("still_scale", [P, P], U8)
-        nc.vector.memset(zeros[:].bitcast(I32), 0)
-        nc.vector.memset(a4_plane[:].bitcast(I32), 0)
-        for c0 in (0, BANK // 2):
-            cols = slice(c0, c0 + BANK // 2)
-            nc.vector.quantize_mx(out=warm_codes[:, cols].bitcast(E4M3), scales=warm_scale[:, cols], in_=zeros[:])
-        nc.vector.quantize_mx(out=still_codes[:].bitcast(E5M2), scales=still_scale[:], in_=zeros[:, 0:BANK])
-        for plane in (a8_plane, b4_plane, b8_plane):
+        for plane in (a4_plane, a8_plane, b4_plane, b8_plane):
             nc.vector.memset(plane[:].bitcast(I32), 0)
 
         def load_scales(plane, scales):
@@ -224,17 +212,6 @@ def tile_mix_kfac_mix_res_sgd_kernel(
         def store_pair(pair):
             nc.sync.dma_start(
                 out=out[2 * pair * P : 2 * (pair + 1) * P, :].rearrange("(p e) n -> p e n", e=2), in_=res[pair][:]
-            )
-
-        for i in range(WARM):
-            nc.tensor.matmul_mx(
-                out=banks[7][:],
-                lhsT=still_codes[:].bitcast(E5M2),
-                lhsT_scale=still_scale[:],
-                rhs=warm_codes[:].bitcast(E4M3),
-                rhs_scale=warm_scale[:],
-                start=True,
-                stop=True,
             )
 
         cast_g_shared(1, 0, 0, 88, P)

@@ -20,7 +20,7 @@ PACK = 4
 PASS = P * PACK
 BANK = 512
 STEP = -0.0625
-HALF = P // 2
+CUT = 3 * P // 4
 
 
 def tile_mix_kfac_mix_res_sgd_kernel(
@@ -81,8 +81,8 @@ def tile_mix_kfac_mix_res_sgd_kernel(
         a8 = load_fp8("a8", a8_words[0])
         load_scales(a8_plane, a8_scales)
         for kh in (1, 0):
-            load_g(kh, 1, 0, HALF)
-            load_g(kh, 1, HALF, P)
+            load_g(kh, 1, 0, CUT)
+            load_g(kh, 1, CUT, P)
         b4 = tile("b4", [P, 2, 2 * N], U8)
         nc.sync.dma_start(out=b4[:].bitcast(I32), in_=b4_words.rearrange("a p w -> p a w").bitcast(I32))
         load_scales(b4_plane, b4_scales)
@@ -225,12 +225,13 @@ def tile_mix_kfac_mix_res_sgd_kernel(
         drain_h(nc.scalar, 0, 0, 0)
         drain_h(nc.vector, 0, 0, 1)
         drain_h(nc.scalar, 0, 0, 2)
-        cast_g(nc.vector, 1, 1, 0, 0, HALF)
+        cast_g(nc.vector, 1, 1, 0, 0, CUT, 0, 2)
         drain_h(nc.scalar, 0, 0, 3)
-        cast_g(nc.vector, 1, 1, HALF, HALF, P, 0, 2)
-        cast_g(nc.vector, 1, 1, HALF, HALF, HALF + 32, 2, PACK)
+        cast_g(nc.vector, 1, 1, CUT, CUT, P, 0, 2)
+        cast_g(nc.vector, 1, 1, 0, 0, CUT // 2, 2, PACK)
         quantize_g(1, 1, 0, 2)
-        cast_g(nc.vector, 1, 1, HALF, HALF + 32, P, 2, PACK)
+        cast_g(nc.vector, 1, 1, 0, CUT // 2, CUT, 2, PACK)
+        cast_g(nc.vector, 1, 1, CUT, CUT, P, 2, PACK)
         for j in range(PACK):
             drain_h(nc.scalar, 0, 1, j)
         quantize_g(1, 1, 2, PACK)
@@ -238,11 +239,17 @@ def tile_mix_kfac_mix_res_sgd_kernel(
         first_product(1, 1, 1, 0, 1)
         first_product(1, 1, 0, 2, PACK)
         first_product(1, 1, 1, 1, PACK)
-        cast_g(nc.vector, 0, 1, 0, 0, HALF)
-        cast_g_shared(0, 1, HALF, HALF + 24, P)
-        quantize_g(0, 1)
-        first_product(0, 1, 0)
-        first_product(0, 1, 1)
+        cast_g(nc.vector, 0, 1, 0, 0, CUT, 0, 2)
+        cast_g(nc.scalar, 0, 1, 0, 0, 32, 2, PACK)
+        cast_g(nc.vector, 0, 1, CUT, CUT, P, 0, 2)
+        cast_g(nc.vector, 0, 1, 0, 32, CUT, 2, PACK)
+        quantize_g(0, 1, 0, 2)
+        cast_g(nc.vector, 0, 1, CUT, CUT, P, 2, PACK)
+        quantize_g(0, 1, 2, PACK)
+        first_product(0, 1, 0, 0, 2)
+        first_product(0, 1, 1, 0, 1)
+        first_product(0, 1, 0, 2, PACK)
+        first_product(0, 1, 1, 1, PACK)
         interleave_h(nc.vector, 0, 0, 2)
         quantize_h(0, 0, 2)
         for j in range(3):

@@ -241,6 +241,7 @@ def tile_mix_kfac_mix_res_sgd_kernel(
         first_product(1, 1, 1, 1, PACK)
         cast_g(nc.vector, 0, 1, 0, 0, CUT, 0, 2)
         cast_g(nc.scalar, 0, 1, 0, 0, 32, 2, PACK)
+        interleave_h(nc.scalar, 0, 0, 2)
         cast_g(nc.vector, 0, 1, CUT, CUT, P, 0, 2)
         cast_g(nc.vector, 0, 1, 0, 32, CUT, 2, PACK)
         quantize_g(0, 1, 0, 2)
@@ -250,41 +251,46 @@ def tile_mix_kfac_mix_res_sgd_kernel(
         first_product(0, 1, 1, 0, 1)
         first_product(0, 1, 0, 2, PACK)
         first_product(0, 1, 1, 1, PACK)
-        interleave_h(nc.vector, 0, 0, 2)
         quantize_h(0, 0, 2)
-        for j in range(3):
-            drain_h(nc.scalar, 1, 0, j)
-        drain_h(nc.vector, 1, 0, 3)
+        for j in range(PACK):
+            drain_h(nc.vector if j % 2 else nc.scalar, 1, 0, j)
         for j in range(PACK):
             drain_h(nc.scalar, 1, 1, j)
-        interleave_h(nc.vector, 1, 0, 2)
         interleave_h(nc.vector, 0, 2, 2)
-        quantize_h(1, 0, 2)
-        interleave_h(nc.vector, 1, 2, 2)
+        interleave_h(nc.vector, 1, 0, 2)
         quantize_h(0, 2, 2)
+        interleave_h(nc.vector, 1, 2, 2)
+        quantize_h(1, 0, 2)
+        quantize_h(1, 2, 2)
         for mt0 in (4, 6):
             for lh in range(2):
                 interleave_h(nc.scalar, lh, mt0, 2)
 
-        for lh in range(2):
-            for tier in range(2):
-                for mt in range(2):
-                    for nh in range(2):
-                        second_product(mt, nh, lh, tier, lh == 0 and tier == 0, lh == 1 and tier == 1)
-        quantize_h(1, 2, 2)
-        for mt in range(2):
+        one_stationary = [(0, 0), (0, 1), (1, 1), (1, 0)]
+        for tier in range(2):
+            for mt in range(2):
+                for nh in range(2):
+                    second_product(mt, nh, 0, tier, tier == 0, False)
+        for mt in range(2, 4):
+            for tier, nh in one_stationary:
+                second_product(mt, nh, 0, tier, tier == 0, False)
+        for mt in range(4):
+            for nh in range(2):
+                for tier in (nh, 1 - nh):
+                    second_product(mt, nh, 1, tier, False, tier != nh)
             update(mt, 0)
             update(mt, 1)
-        store_pair(0)
+            if mt % 2 == 1:
+                store_pair(mt // 2)
+            if mt in (0, 2):
+                for lh in range(2):
+                    quantize_h(lh, 4 + mt, 2)
         last = M // P - 1
-        for mt in range(2, M // P):
+        for mt in range(4, M // P):
             there = [(0, 0), (0, 1), (1, 1), (1, 0)]
             for nh in range(2):
                 for i, (lh, tier) in enumerate(there if nh == 0 else there[::-1]):
                     second_product(mt, nh, lh, tier, i == 0, i == 3)
-            if mt in (2, 3):
-                for lh in range(2):
-                    quantize_h(lh, 2 * mt, 2)
             update(mt, 0)
             if mt >= last - 1:
                 store(mt, 0, BANK)
@@ -297,7 +303,5 @@ def tile_mix_kfac_mix_res_sgd_kernel(
                 update(mt, 1)
                 if mt == last - 1:
                     store(mt, BANK, N)
-                elif mt >= 4:
+                else:
                     store(mt, 0, N)
-                elif mt % 2 == 1:
-                    store_pair(mt // 2)

@@ -37,12 +37,15 @@ def tile_mix_kfac_mix_res_sgd_kernel(
 
         banks = [psum.tile([P, BANK], F32, name="bank%d" % i) for i in range(8)]
 
-        a8_plane = tile("a8_plane", [P, 1, M], U8)
-        a4_plane = tile("a4_plane", [P, 1, M], U8)
-        b4_plane = tile("b4_plane", [P, 2, N], U8)
-        b8_plane = tile("b8_plane", [P, 2, N], U8)
+        def shifted(name, width, dtype, skip):
+            return tile(name, [P, skip + width], dtype)[:, skip:]
+
+        a8_plane = shifted("a8_plane", M, U8, 128).rearrange("p (a n) -> p a n", a=1)
+        a4_plane = shifted("a4_plane", M, U8, 128).rearrange("p (a n) -> p a n", a=1)
+        b4_plane = shifted("b4_plane", 2 * N, U8, 128).rearrange("p (a n) -> p a n", a=2)
+        b8_plane = shifted("b8_plane", 2 * N, U8, 128).rearrange("p (a n) -> p a n", a=2)
         for plane in (a4_plane, a8_plane, b4_plane, b8_plane):
-            nc.vector.memset(plane[:].bitcast(I32), 0)
+            nc.vector.memset(plane.bitcast(I32), 0)
 
         def load_scales(plane, scales):
             for r in range(4):
@@ -118,8 +121,8 @@ def tile_mix_kfac_mix_res_sgd_kernel(
 
         def quantize_g(kh, lh, j0=0, j1=PACK):
             for j in range(j0, j1):
-                codes = tile("g_codes%d%d%d" % (kh, lh, j), [P, P], I32)
-                scale = tile("g_scale%d%d%d" % (kh, lh, j), [P, P], U8)
+                codes = shifted("g_codes%d%d%d" % (kh, lh, j), P, I32, 16)
+                scale = shifted("g_scale%d%d%d" % (kh, lh, j), P, U8, 192)
                 nc.vector.quantize_mx(
                     out=codes[:].bitcast(E5M2),
                     scales=scale[:],
@@ -127,22 +130,23 @@ def tile_mix_kfac_mix_res_sgd_kernel(
                 )
                 g_codes[kh, lh, j], g_scale[kh, lh, j] = codes, scale
 
-        def first_product(kh, lh, mh, j0=0, j1=PACK):
-            cols = slice(mh * BANK, (mh + 1) * BANK)
-            if kh == 0:
-                rhs, rhs_scale = a8[:, cols].bitcast(E4M3), a8_plane[:, 0, cols]
-            else:
-                rhs, rhs_scale = a4[:, 2 * cols.start : 2 * cols.stop].bitcast(E2M1), a4_plane[:, 0, cols]
-            for j in range(j0, j1):
-                nc.tensor.matmul_mx(
-                    out=banks[PACK * mh + j][:],
-                    lhsT=g_codes[kh, lh, j][:].bitcast(E5M2),
-                    lhsT_scale=g_scale[kh, lh, j][:],
-                    rhs=rhs,
-                    rhs_scale=rhs_scale,
-                    start=(kh == 1),
-                    stop=(kh == 0),
-                )
+        def first_product(kh, lh):
+            for j in range(PACK):
+                for mh in range(2):
+                    cols = slice(mh * BANK, (mh + 1) * BANK)
+                    if kh == 0:
+                        rhs, rhs_scale = a8[:, cols].bitcast(E4M3), a8_plane[:, 0, cols]
+                    else:
+                        rhs, rhs_scale = a4[:, 2 * cols.start : 2 * cols.stop].bitcast(E2M1), a4_plane[:, 0, cols]
+                    nc.tensor.matmul_mx(
+                        out=banks[PACK * mh + j][:],
+                        lhsT=g_codes[kh, lh, j][:].bitcast(E5M2),
+                        lhsT_scale=g_scale[kh, lh, j][:],
+                        rhs=rhs,
+                        rhs_scale=rhs_scale,
+                        start=(kh == 1),
+                        stop=(kh == 0),
+                    )
 
         h_rows = {(lh, mh): tile("h_rows%d%d" % (lh, mh), [P, PACK, BANK], BF16) for lh in range(2) for mh in range(2)}
         h_bf, h_codes, h_scale = {}, {}, {}
@@ -163,8 +167,8 @@ def tile_mix_kfac_mix_res_sgd_kernel(
 
         def quantize_h(lh, mt0, count):
             for i in range(count):
-                codes = tile("h_codes%d%d" % (lh, mt0 + i), [P, P], I32)
-                scale = tile("h_scale%d%d" % (lh, mt0 + i), [P, P], U8)
+                codes = shifted("h_codes%d%d" % (lh, mt0 + i), P, I32, 16)
+                scale = shifted("h_scale%d%d" % (lh, mt0 + i), P, U8, 192)
                 nc.vector.quantize_mx(
                     out=codes[:].bitcast(E5M2),
                     scales=scale[:],
@@ -174,7 +178,7 @@ def tile_mix_kfac_mix_res_sgd_kernel(
                 h_scale[lh, mt0 + i] = scale[:]
 
         def y_bank(mt, nh):
-            return banks[(2 * mt + nh) % 8]
+            return banks[PACK * nh + mt % PACK]
 
         def second_product(mt, nh, lh, tier, start, stop):
             cols = slice(nh * BANK, (nh + 1) * BANK)
@@ -216,49 +220,38 @@ def tile_mix_kfac_mix_res_sgd_kernel(
 
         cast_g_shared(1, 0, 0, 88, P)
         quantize_g(1, 0)
-        first_product(1, 0, 0)
-        first_product(1, 0, 1)
+        first_product(1, 0)
         cast_g_shared(0, 0, 0, 88, P)
         quantize_g(0, 0)
-        first_product(0, 0, 0)
-        first_product(0, 0, 1)
-        drain_h(nc.scalar, 0, 0, 0)
-        drain_h(nc.vector, 0, 0, 1)
-        drain_h(nc.scalar, 0, 0, 2)
-        cast_g(nc.vector, 1, 1, 0, 0, CUT, 0, 2)
-        drain_h(nc.scalar, 0, 0, 3)
-        cast_g(nc.vector, 1, 1, CUT, CUT, P, 0, 2)
-        cast_g(nc.vector, 1, 1, 0, 0, CUT // 2, 2, PACK)
-        quantize_g(1, 1, 0, 2)
-        cast_g(nc.vector, 1, 1, 0, CUT // 2, CUT, 2, PACK)
-        cast_g(nc.vector, 1, 1, CUT, CUT, P, 2, PACK)
+        first_product(0, 0)
         for j in range(PACK):
-            drain_h(nc.scalar, 0, 1, j)
-        quantize_g(1, 1, 2, PACK)
-        first_product(1, 1, 0, 0, 2)
-        first_product(1, 1, 1, 0, 1)
-        first_product(1, 1, 0, 2, PACK)
-        first_product(1, 1, 1, 1, PACK)
-        cast_g(nc.vector, 0, 1, 0, 0, CUT, 0, 2)
-        cast_g(nc.scalar, 0, 1, 0, 0, 32, 2, PACK)
+            for mh in range(2):
+                drain_h(nc.vector if (mh, j) == (1, 0) else nc.scalar, 0, mh, j)
+
+        def round_in_pieces(kh, shared, filler):
+            cast_g(nc.vector, kh, 1, 0, 0, CUT, 0, 2)
+            cast_g(nc.vector, kh, 1, CUT, CUT, P, 0, 2)
+            cast_g(nc.vector, kh, 1, 0, shared, filler, 2, PACK)
+            quantize_g(kh, 1, 0, 1)
+            if filler < CUT:
+                cast_g(nc.vector, kh, 1, 0, filler, CUT, 2, PACK)
+            cast_g(nc.vector, kh, 1, CUT, CUT, P, 2, PACK)
+            quantize_g(kh, 1, 1, PACK)
+            first_product(kh, 1)
+
+        round_in_pieces(1, 0, 40)
+        cast_g(nc.scalar, 0, 1, 0, 0, 56, 2, PACK)
         interleave_h(nc.scalar, 0, 0, 2)
-        cast_g(nc.vector, 0, 1, CUT, CUT, P, 0, 2)
-        cast_g(nc.vector, 0, 1, 0, 32, CUT, 2, PACK)
-        quantize_g(0, 1, 0, 2)
-        cast_g(nc.vector, 0, 1, CUT, CUT, P, 2, PACK)
-        quantize_g(0, 1, 2, PACK)
-        first_product(0, 1, 0, 0, 2)
-        first_product(0, 1, 1, 0, 1)
-        first_product(0, 1, 0, 2, PACK)
-        first_product(0, 1, 1, 1, PACK)
+        round_in_pieces(0, 56, CUT)
         quantize_h(0, 0, 2)
-        for j in range(PACK):
-            drain_h(nc.vector if j % 2 else nc.scalar, 1, 0, j)
-        for j in range(PACK):
-            drain_h(nc.scalar, 1, 1, j)
+        drain_h(nc.scalar, 1, 0, 0)
+        drain_h(nc.vector, 1, 1, 0)
         interleave_h(nc.vector, 0, 2, 2)
-        interleave_h(nc.vector, 1, 0, 2)
+        for mh, j in ((0, 1), (1, 1), (0, 2), (1, 2), (1, 3)):
+            drain_h(nc.scalar, 1, mh, j)
+        drain_h(nc.vector, 1, 0, 3)
         quantize_h(0, 2, 2)
+        interleave_h(nc.vector, 1, 0, 2)
         interleave_h(nc.vector, 1, 2, 2)
         quantize_h(1, 0, 2)
         quantize_h(1, 2, 2)

@@ -180,14 +180,14 @@ def tile_mix_kfac_mix_res_sgd_kernel(
         def y_bank(mt, nh):
             return banks[PACK * nh + mt % PACK]
 
-        def second_product(mt, nh, lh, tier, start, stop):
-            cols = slice(nh * BANK, (nh + 1) * BANK)
+        def second_product(mt, nh, lh, tier, start, stop, c0=0, c1=BANK, bank=None):
+            cols = slice(nh * BANK + c0, nh * BANK + c1)
             if tier == 0:
                 rhs, rhs_scale = b4[:, lh, 2 * cols.start : 2 * cols.stop].bitcast(E2M1), b4_plane[:, lh, cols]
             else:
                 rhs, rhs_scale = b8[lh][:, cols].bitcast(E4M3), b8_plane[:, lh, cols]
             nc.tensor.matmul_mx(
-                out=y_bank(mt, nh)[:],
+                out=y_bank(mt, nh)[:] if bank is None else bank[:, : c1 - c0],
                 lhsT=h_codes[lh, mt].bitcast(E5M2),
                 lhsT_scale=h_scale[lh, mt],
                 rhs=rhs,
@@ -198,11 +198,11 @@ def tile_mix_kfac_mix_res_sgd_kernel(
 
         res = [tile("res%d" % pair, [P, 2, N], F32) for pair in range(M // (2 * P))]
 
-        def update(mt, nh, c0=0, c1=BANK):
+        def update(mt, nh, c0=0, c1=BANK, bank=None):
             cols = slice(nh * BANK + c0, nh * BANK + c1)
             nc.vector.scalar_tensor_tensor(
                 out=res[mt // 2][:, mt % 2, cols],
-                in0=y_bank(mt, nh)[:, c0:c1],
+                in0=y_bank(mt, nh)[:, c0:c1] if bank is None else bank[:, : c1 - c0],
                 scalar=STEP,
                 in1=prm_sb[mt // 2][:, mt % 2, cols],
                 op0=MULT,
@@ -279,22 +279,26 @@ def tile_mix_kfac_mix_res_sgd_kernel(
                 for lh in range(2):
                     quantize_h(lh, 4 + mt, 2)
         last = M // P - 1
-        for mt in range(4, M // P):
-            there = [(0, 0), (0, 1), (1, 1), (1, 0)]
+        there = [(0, 0), (0, 1), (1, 1), (1, 0)]
+        for mt in range(4, last):
             for nh in range(2):
                 for i, (lh, tier) in enumerate(there if nh == 0 else there[::-1]):
                     second_product(mt, nh, lh, tier, i == 0, i == 3)
             update(mt, 0)
-            if mt >= last - 1:
+            if mt == last - 1:
                 store(mt, 0, BANK)
-            if mt == last:
-                update(mt, 1, 0, BANK // 2)
-                store(mt, BANK, BANK + BANK // 2)
-                update(mt, 1, BANK // 2, BANK)
-                store(mt, BANK + BANK // 2, N)
+                update(mt, 1)
+                store(mt, BANK, N)
             else:
                 update(mt, 1)
-                if mt == last - 1:
-                    store(mt, BANK, N)
-                else:
-                    store(mt, 0, N)
+                store(mt, 0, N)
+        pieces = [(0, 256, 3), (256, 512, 7), (512, 768, 0), (768, 896, 4), (896, N, 1)]
+        stored = 0
+        for k, (c0, c1, bank) in enumerate(pieces):
+            nh = c0 // BANK
+            for i, (lh, tier) in enumerate(there if k % 2 == 0 else there[::-1]):
+                second_product(last, nh, lh, tier, i == 0, i == 3, c0 - nh * BANK, c1 - nh * BANK, banks[bank])
+            update(last, nh, c0 - nh * BANK, c1 - nh * BANK, banks[bank])
+            if c1 in (512, 768, N):
+                store(last, stored, c1)
+                stored = c1

@@ -8,6 +8,7 @@ FLOPS = 2 * K * L * M + 2 * 2 * L * M * N
 F32 = mybir.dt.float32
 BF16 = mybir.dt.bfloat16
 I32 = mybir.dt.int32
+U32 = mybir.dt.uint32
 U8 = mybir.dt.uint8
 E4M3 = mybir.dt.float8_e4m3fn_x4
 E5M2 = mybir.dt.float8_e5m2_x4
@@ -19,8 +20,15 @@ P = 128
 PACK = 4
 PASS = P * PACK
 BANK = 512
+QUARTER = 256
 STEP = -0.0625
 CUT = 3 * P // 4
+SHARE_WHOLE = 88
+SHARE_LAST = 56
+FILL = 40
+TILES = M // P
+PRM_LOADS = [(0, 3), (3, 5), (5, 8)]
+STORE_ENDS = [3 * N, 5 * N, 6 * N + 512, 7 * N + 256, 7 * N + 768, 8 * N]
 
 
 def tile_mix_kfac_mix_res_sgd_kernel(
@@ -40,8 +48,8 @@ def tile_mix_kfac_mix_res_sgd_kernel(
         def shifted(name, width, dtype, skip):
             return tile(name, [P, skip + width], dtype)[:, skip:]
 
-        a8_plane = shifted("a8_plane", M, U8, 128).rearrange("p (a n) -> p a n", a=1)
-        a4_plane = shifted("a4_plane", M, U8, 128).rearrange("p (a n) -> p a n", a=1)
+        a_planes = shifted("a_planes", 2 * M, U8, 128).rearrange("p (a n) -> p a n", a=2)
+        a4_plane, a8_plane = a_planes[:, 0:1, :], a_planes[:, 1:2, :]
         b4_plane = shifted("b4_plane", 2 * N, U8, 128).rearrange("p (a n) -> p a n", a=2)
         b8_plane = shifted("b8_plane", 2 * N, U8, 128).rearrange("p (a n) -> p a n", a=2)
         for plane in (a4_plane, a8_plane, b4_plane, b8_plane):
@@ -56,10 +64,10 @@ def tile_mix_kfac_mix_res_sgd_kernel(
 
         g_raw = {}
 
-        def load_g(kh, lh, c0, c1):
+        def load_g(kh, lh, c0, c1, queue=nc.sync):
             raw = tile("g_raw%d%d_%d" % (kh, lh, c0), [P, PACK, PACK * (c1 - c0)], F32)
             l0 = lh * PASS
-            nc.sync.dma_start(
+            queue.dma_start(
                 out=raw[:],
                 in_=g[kh * PASS : (kh + 1) * PASS, l0 + PACK * c0 : l0 + PACK * c1].rearrange(
                     "(p t) w -> p t w", t=PACK
@@ -77,28 +85,31 @@ def tile_mix_kfac_mix_res_sgd_kernel(
             nc.sync.dma_start(out=dst[:].bitcast(I32), in_=words.bitcast(I32))
             return dst
 
-        load_g(1, 0, 0, P)
+        load_g(1, 0, 0, P, nc.scalar)
+        for plane, scales in ((a4_plane, a4_scales), (a8_plane, a8_scales)):
+            nc.sync.dma_start(out=plane[0:P:8, 0, :].bitcast(I32), in_=scales[0].bitcast(I32))
+        for r in range(1, 4):
+            nc.sync.dma_start(out=a_planes[r:P:32].bitcast(I32), in_=a_planes[8 * r : P : 32].bitcast(I32))
         a4 = load_fp4("a4", a4_words[0])
-        load_scales(a4_plane, a4_scales)
         load_g(0, 0, 0, P)
         a8 = load_fp8("a8", a8_words[0])
-        load_scales(a8_plane, a8_scales)
         for kh in (1, 0):
             load_g(kh, 1, 0, CUT)
             load_g(kh, 1, CUT, P)
         b4 = tile("b4", [P, 2, 2 * N], U8)
         nc.sync.dma_start(out=b4[:].bitcast(I32), in_=b4_words.rearrange("a p w -> p a w").bitcast(I32))
         load_scales(b4_plane, b4_scales)
-        b8 = [load_fp8("b8_0", b8_words[0])]
+        b8 = tile("b8", [P, 2, N], I32)
+        nc.sync.dma_start(out=b8[:], in_=b8_words.rearrange("a p n t -> p a (n t)").bitcast(I32))
         load_scales(b8_plane, b8_scales)
-        b8.append(load_fp8("b8_1", b8_words[1]))
-        prm_sb = []
-        for pair in range(M // (2 * P)):
-            rows = tile("prm%d" % pair, [P, 2, N], F32)
-            nc.sync.dma_start(
-                out=rows[:], in_=prm[2 * pair * P : 2 * (pair + 1) * P, :].rearrange("(p e) n -> p e n", e=2)
-            )
-            prm_sb.append(rows)
+        prm_rows = prm.rearrange("(p e) n -> p (e n)", e=TILES)
+        out_rows = out.rearrange("(p e) n -> p (e n)", e=TILES)
+        prm_sb = {}
+        for t0, t1 in PRM_LOADS:
+            rows = tile("prm%d" % t0, [P, (t1 - t0) * N], F32)
+            nc.sync.dma_start(out=rows[:], in_=prm_rows[:, t0 * N : t1 * N])
+            for mt in range(t0, t1):
+                prm_sb[mt] = rows[:, (mt - t0) * N : (mt - t0 + 1) * N]
 
         g_bf = {(kh, lh): tile("g_bf%d%d" % (kh, lh), [P, PACK, P, PACK], BF16) for kh in range(2) for lh in range(2)}
         g_codes, g_scale = {}, {}
@@ -114,11 +125,6 @@ def tile_mix_kfac_mix_res_sgd_kernel(
             src = g_raw[kh, lh, first][:, :, PACK * (c0 - first) : PACK * (c1 - first)]
             copy(engine, dst, src.rearrange("p t (c j) -> p c t j", j=PACK)[:, :, :, j0:j1])
 
-        def cast_g_shared(kh, lh, c0, split, c1):
-            cast_g(nc.scalar, kh, lh, c0, c0, split, 2, PACK)
-            cast_g(nc.vector, kh, lh, c0, c0, c1, 0, 2)
-            cast_g(nc.vector, kh, lh, c0, split, c1, 2, PACK)
-
         def quantize_g(kh, lh, j0=0, j1=PACK):
             for j in range(j0, j1):
                 codes = shifted("g_codes%d%d%d" % (kh, lh, j), P, I32, 16)
@@ -130,62 +136,68 @@ def tile_mix_kfac_mix_res_sgd_kernel(
                 )
                 g_codes[kh, lh, j], g_scale[kh, lh, j] = codes, scale
 
-        def first_product(kh, lh):
-            for j in range(PACK):
-                for mh in range(2):
-                    cols = slice(mh * BANK, (mh + 1) * BANK)
-                    if kh == 0:
-                        rhs, rhs_scale = a8[:, cols].bitcast(E4M3), a8_plane[:, 0, cols]
-                    else:
-                        rhs, rhs_scale = a4[:, 2 * cols.start : 2 * cols.stop].bitcast(E2M1), a4_plane[:, 0, cols]
-                    nc.tensor.matmul_mx(
-                        out=banks[PACK * mh + j][:],
-                        lhsT=g_codes[kh, lh, j][:].bitcast(E5M2),
-                        lhsT_scale=g_scale[kh, lh, j][:],
-                        rhs=rhs,
-                        rhs_scale=rhs_scale,
-                        start=(kh == 1),
-                        stop=(kh == 0),
-                    )
+        def h_bank(jp, q):
+            return banks[PACK * jp + q]
 
-        h_rows = {(lh, mh): tile("h_rows%d%d" % (lh, mh), [P, PACK, BANK], BF16) for lh in range(2) for mh in range(2)}
+        def first_product(kh, lh):
+            for jp in range(2):
+                for q in range(4):
+                    for jj in range(2):
+                        cols = slice(q * QUARTER, (q + 1) * QUARTER)
+                        if kh == 0:
+                            rhs, rhs_scale = a8[:, cols].bitcast(E4M3), a8_plane[:, 0, cols]
+                        else:
+                            rhs = a4[:, 2 * cols.start : 2 * cols.stop].bitcast(E2M1)
+                            rhs_scale = a4_plane[:, 0, cols]
+                        nc.tensor.matmul_mx(
+                            out=h_bank(jp, q)[:, jj * QUARTER : (jj + 1) * QUARTER],
+                            lhsT=g_codes[kh, lh, 2 * jp + jj][:].bitcast(E5M2),
+                            lhsT_scale=g_scale[kh, lh, 2 * jp + jj][:],
+                            rhs=rhs,
+                            rhs_scale=rhs_scale,
+                            start=(kh == 1 and jj == 0),
+                            stop=(kh == 0 and jj == 1),
+                        )
+
+        h_pairs = [tile("h_pairs%d" % lh, [P, 2, 2 * M], BF16) for lh in range(2)]
         h_bf, h_codes, h_scale = {}, {}, {}
 
-        def drain_h(engine, lh, mh, j):
-            copy(engine, h_rows[lh, mh][:, j, :], banks[PACK * mh + j][:])
-
-        def interleave_h(engine, lh, mt0, count):
-            dst = tile("h_bf%d%d" % (lh, mt0), [P, count * P, PACK], BF16)
-            c0 = (mt0 % 4) * P
-            src = h_rows[lh, mt0 // 4][:, :, c0 : c0 + count * P]
+        def drain_h(engine, lh, jp, q):
+            c = QUARTER // TILES
             copy(
                 engine,
-                dst[:].rearrange("p (e c q) j -> p c j q e", e=2, q=2),
-                src.rearrange("p j (c q e) -> p c j q e", e=2, q=2),
+                h_pairs[lh][:, jp, :].rearrange("p (e c j) -> p e c j", e=TILES, j=2)[:, :, q * c : (q + 1) * c, :],
+                h_bank(jp, q)[:].rearrange("p (j c e) -> p e c j", j=2, e=TILES),
             )
-            h_bf[lh, mt0] = dst
 
-        def quantize_h(lh, mt0, count):
-            for i in range(count):
-                codes = shifted("h_codes%d%d" % (lh, mt0 + i), P, I32, 16)
-                scale = shifted("h_scale%d%d" % (lh, mt0 + i), P, U8, 192)
-                nc.vector.quantize_mx(
-                    out=codes[:].bitcast(E5M2),
-                    scales=scale[:],
-                    in_=h_bf[lh, mt0][:, i * P : (i + 1) * P, :].rearrange("p c j -> p (c j)"),
-                )
-                h_codes[lh, mt0 + i] = codes[:]
-                h_scale[lh, mt0 + i] = scale[:]
+        def interleave_h(engine, lh, q):
+            word = U32 if engine is nc.scalar else I32
+            dst = tile("h_bf%d%d" % (lh, q), [P, QUARTER * PACK], BF16)
+            src = h_pairs[lh][:].bitcast(word)[:, :, q * QUARTER : (q + 1) * QUARTER]
+            copy(
+                engine,
+                dst[:].bitcast(word).rearrange("p (c i j) -> p c j i", i=2, j=2),
+                src.rearrange("p j (c i) -> p c j i", i=2),
+            )
+            h_bf[lh, q] = dst
+
+        def quantize_h(lh, q):
+            codes = shifted("h_codes%d%d" % (lh, q), QUARTER, I32, 16)
+            scale = shifted("h_scale%d%d" % (lh, q), QUARTER, U8, 192)
+            nc.vector.quantize_mx(out=codes[:].bitcast(E5M2), scales=scale[:], in_=h_bf[lh, q][:])
+            for e in range(2):
+                h_codes[lh, 2 * q + e] = codes[:, e * P : (e + 1) * P]
+                h_scale[lh, 2 * q + e] = scale[:, e * P : (e + 1) * P]
 
         def y_bank(mt, nh):
-            return banks[PACK * nh + mt % PACK]
+            return banks[2 * (mt % 4) + nh]
 
         def second_product(mt, nh, lh, tier, start, stop, c0=0, c1=BANK, bank=None):
             cols = slice(nh * BANK + c0, nh * BANK + c1)
             if tier == 0:
                 rhs, rhs_scale = b4[:, lh, 2 * cols.start : 2 * cols.stop].bitcast(E2M1), b4_plane[:, lh, cols]
             else:
-                rhs, rhs_scale = b8[lh][:, cols].bitcast(E4M3), b8_plane[:, lh, cols]
+                rhs, rhs_scale = b8[:, lh, cols].bitcast(E4M3), b8_plane[:, lh, cols]
             nc.tensor.matmul_mx(
                 out=y_bank(mt, nh)[:] if bank is None else bank[:, : c1 - c0],
                 lhsT=h_codes[lh, mt].bitcast(E5M2),
@@ -196,88 +208,79 @@ def tile_mix_kfac_mix_res_sgd_kernel(
                 stop=stop,
             )
 
-        res = [tile("res%d" % pair, [P, 2, N], F32) for pair in range(M // (2 * P))]
+        res = tile("res", [P, TILES * N], F32)
+        stored = [0]
 
         def update(mt, nh, c0=0, c1=BANK, bank=None):
-            cols = slice(nh * BANK + c0, nh * BANK + c1)
+            n0, n1 = nh * BANK + c0, nh * BANK + c1
             nc.vector.scalar_tensor_tensor(
-                out=res[mt // 2][:, mt % 2, cols],
+                out=res[:, mt * N + n0 : mt * N + n1],
                 in0=y_bank(mt, nh)[:, c0:c1] if bank is None else bank[:, : c1 - c0],
                 scalar=STEP,
-                in1=prm_sb[mt // 2][:, mt % 2, cols],
+                in1=prm_sb[mt][:, n0:n1],
                 op0=MULT,
                 op1=ADD,
             )
+            end = mt * N + n1
+            if end in STORE_ENDS:
+                nc.sync.dma_start(out=out_rows[:, stored[-1] : end], in_=res[:, stored[-1] : end])
+                stored.append(end)
 
-        def store(mt, c0, c1):
-            rows = out[2 * (mt // 2) * P : 2 * (mt // 2 + 1) * P, :].rearrange("(p e) n -> p e n", e=2)
-            nc.sync.dma_start(out=rows[:, mt % 2, c0:c1], in_=res[mt // 2][:, mt % 2, c0:c1])
+        def round_whole(kh):
+            for j0 in (0, 2):
+                cast_g(nc.scalar, kh, 0, 0, SHARE_WHOLE, P, j0, j0 + 2)
+            cast_g(nc.vector, kh, 0, 0, 0, SHARE_WHOLE, 0, 2)
+            cast_g(nc.vector, kh, 0, 0, 0, FILL, 2, PACK)
+            quantize_g(kh, 0, 0, 2)
+            cast_g(nc.vector, kh, 0, 0, FILL, SHARE_WHOLE, 2, PACK)
+            quantize_g(kh, 0, 2, PACK)
+            first_product(kh, 0)
 
-        def store_pair(pair):
-            nc.sync.dma_start(
-                out=out[2 * pair * P : 2 * (pair + 1) * P, :].rearrange("(p e) n -> p e n", e=2), in_=res[pair][:]
-            )
-
-        cast_g_shared(1, 0, 0, 88, P)
-        quantize_g(1, 0)
-        first_product(1, 0)
-        cast_g_shared(0, 0, 0, 88, P)
-        quantize_g(0, 0)
-        first_product(0, 0)
-        for j in range(PACK):
-            for mh in range(2):
-                drain_h(nc.vector if (mh, j) == (1, 0) else nc.scalar, 0, mh, j)
+        round_whole(1)
+        round_whole(0)
+        for jp in range(2):
+            for q in range(4):
+                drain_h(nc.vector if (jp, q) == (0, 1) else nc.scalar, 0, jp, q)
 
         def round_in_pieces(kh, shared, filler):
             cast_g(nc.vector, kh, 1, 0, 0, CUT, 0, 2)
             cast_g(nc.vector, kh, 1, CUT, CUT, P, 0, 2)
             cast_g(nc.vector, kh, 1, 0, shared, filler, 2, PACK)
-            quantize_g(kh, 1, 0, 1)
+            quantize_g(kh, 1, 0, 2)
             if filler < CUT:
                 cast_g(nc.vector, kh, 1, 0, filler, CUT, 2, PACK)
             cast_g(nc.vector, kh, 1, CUT, CUT, P, 2, PACK)
-            quantize_g(kh, 1, 1, PACK)
+            quantize_g(kh, 1, 2, PACK)
             first_product(kh, 1)
 
-        round_in_pieces(1, 0, 40)
-        cast_g(nc.scalar, 0, 1, 0, 0, 56, 2, PACK)
-        interleave_h(nc.scalar, 0, 0, 2)
-        round_in_pieces(0, 56, CUT)
-        quantize_h(0, 0, 2)
-        drain_h(nc.scalar, 1, 0, 0)
-        drain_h(nc.vector, 1, 1, 0)
-        interleave_h(nc.vector, 0, 2, 2)
-        for mh, j in ((0, 1), (1, 1), (0, 2), (1, 2), (1, 3)):
-            drain_h(nc.scalar, 1, mh, j)
-        drain_h(nc.vector, 1, 0, 3)
-        quantize_h(0, 2, 2)
-        interleave_h(nc.vector, 1, 0, 2)
-        interleave_h(nc.vector, 1, 2, 2)
-        quantize_h(1, 0, 2)
-        quantize_h(1, 2, 2)
-        for mt0 in (4, 6):
-            for lh in range(2):
-                interleave_h(nc.scalar, lh, mt0, 2)
+        round_in_pieces(1, 0, FILL)
+        cast_g(nc.scalar, 0, 1, 0, 0, SHARE_LAST, 2, PACK)
+        interleave_h(nc.scalar, 0, 0)
+        round_in_pieces(0, SHARE_LAST, CUT)
+        quantize_h(0, 0)
+        interleave_h(nc.vector, 0, 1)
+        for jp in range(2):
+            for q in range(4):
+                drain_h(nc.vector if (jp, q) in ((0, 2), (1, 1)) else nc.scalar, 1, jp, q)
+                if (jp, q) == (0, 2):
+                    quantize_h(0, 1)
+        quarters = [(lh, q) for lh in range(2) for q in range(4)][2:]
+        interleave_h(nc.vector, *quarters[0])
+        for now, following in zip(quarters, quarters[1:] + [None]):
+            if following:
+                interleave_h(nc.vector, *following)
+            quantize_h(*now)
 
-        one_stationary = [(0, 0), (0, 1), (1, 1), (1, 0)]
         for tier in range(2):
-            for mt in range(2):
+            for mt in range(4):
                 for nh in range(2):
                     second_product(mt, nh, 0, tier, tier == 0, False)
-        for mt in range(2, 4):
-            for tier, nh in one_stationary:
-                second_product(mt, nh, 0, tier, tier == 0, False)
         for mt in range(4):
             for nh in range(2):
                 for tier in (nh, 1 - nh):
                     second_product(mt, nh, 1, tier, False, tier != nh)
             update(mt, 0)
             update(mt, 1)
-            if mt % 2 == 1:
-                store_pair(mt // 2)
-            if mt in (0, 2):
-                for lh in range(2):
-                    quantize_h(lh, 4 + mt, 2)
         last = M // P - 1
         there = [(0, 0), (0, 1), (1, 1), (1, 0)]
         for mt in range(4, last):
@@ -285,20 +288,10 @@ def tile_mix_kfac_mix_res_sgd_kernel(
                 for i, (lh, tier) in enumerate(there if nh == 0 else there[::-1]):
                     second_product(mt, nh, lh, tier, i == 0, i == 3)
             update(mt, 0)
-            if mt == last - 1:
-                store(mt, 0, BANK)
-                update(mt, 1)
-                store(mt, BANK, N)
-            else:
-                update(mt, 1)
-                store(mt, 0, N)
-        pieces = [(0, 256, 3), (256, 512, 7), (512, 768, 0), (768, 896, 4), (896, N, 1)]
-        stored = 0
+            update(mt, 1)
+        pieces = [(0, 256, 6), (256, 512, 7), (512, 768, 0), (768, 896, 1), (896, N, 2)]
         for k, (c0, c1, bank) in enumerate(pieces):
             nh = c0 // BANK
             for i, (lh, tier) in enumerate(there if k % 2 == 0 else there[::-1]):
                 second_product(last, nh, lh, tier, i == 0, i == 3, c0 - nh * BANK, c1 - nh * BANK, banks[bank])
             update(last, nh, c0 - nh * BANK, c1 - nh * BANK, banks[bank])
-            if c1 in (512, 768, N):
-                store(last, stored, c1)
-                stored = c1

@@ -28,7 +28,7 @@ SHARE_LAST = 56
 FILL = 40
 TILES = M // P
 PRM_LOADS = [(0, 3), (3, 5), (5, 8)]
-STORE_ENDS = [3 * N, 5 * N, 6 * N + 512, 7 * N + 256, 7 * N + 768, 8 * N]
+STORE_ENDS = [3 * N, 5 * N, 6 * N, 6 * N + 512, 7 * N, 7 * N + 512, 7 * N + 768, 8 * N]
 
 
 def tile_mix_kfac_mix_res_sgd_kernel(
@@ -64,10 +64,10 @@ def tile_mix_kfac_mix_res_sgd_kernel(
 
         g_raw = {}
 
-        def load_g(kh, lh, c0, c1, queue=nc.sync):
+        def load_g(kh, lh, c0, c1):
             raw = tile("g_raw%d%d_%d" % (kh, lh, c0), [P, PACK, PACK * (c1 - c0)], F32)
             l0 = lh * PASS
-            queue.dma_start(
+            nc.sync.dma_start(
                 out=raw[:],
                 in_=g[kh * PASS : (kh + 1) * PASS, l0 + PACK * c0 : l0 + PACK * c1].rearrange(
                     "(p t) w -> p t w", t=PACK
@@ -85,23 +85,21 @@ def tile_mix_kfac_mix_res_sgd_kernel(
             nc.sync.dma_start(out=dst[:].bitcast(I32), in_=words.bitcast(I32))
             return dst
 
-        load_g(1, 0, 0, P, nc.scalar)
-        for plane, scales in ((a4_plane, a4_scales), (a8_plane, a8_scales)):
-            nc.sync.dma_start(out=plane[0:P:8, 0, :].bitcast(I32), in_=scales[0].bitcast(I32))
-        for r in range(1, 4):
-            nc.sync.dma_start(out=a_planes[r:P:32].bitcast(I32), in_=a_planes[8 * r : P : 32].bitcast(I32))
+        load_g(1, 0, 0, P)
         a4 = load_fp4("a4", a4_words[0])
+        load_scales(a4_plane, a4_scales)
         load_g(0, 0, 0, P)
         a8 = load_fp8("a8", a8_words[0])
-        for kh in (1, 0):
-            load_g(kh, 1, 0, CUT)
-            load_g(kh, 1, CUT, P)
+        load_scales(a8_plane, a8_scales)
+        load_g(1, 1, 0, P)
+        load_g(0, 1, 0, CUT)
+        load_g(0, 1, CUT, P)
         b4 = tile("b4", [P, 2, 2 * N], U8)
         nc.sync.dma_start(out=b4[:].bitcast(I32), in_=b4_words.rearrange("a p w -> p a w").bitcast(I32))
         load_scales(b4_plane, b4_scales)
-        b8 = tile("b8", [P, 2, N], I32)
-        nc.sync.dma_start(out=b8[:], in_=b8_words.rearrange("a p n t -> p a (n t)").bitcast(I32))
+        b8 = [load_fp8("b8_0", b8_words[0])]
         load_scales(b8_plane, b8_scales)
+        b8.append(load_fp8("b8_1", b8_words[1]))
         prm_rows = prm.rearrange("(p e) n -> p (e n)", e=TILES)
         out_rows = out.rearrange("(p e) n -> p (e n)", e=TILES)
         prm_sb = {}
@@ -197,7 +195,7 @@ def tile_mix_kfac_mix_res_sgd_kernel(
             if tier == 0:
                 rhs, rhs_scale = b4[:, lh, 2 * cols.start : 2 * cols.stop].bitcast(E2M1), b4_plane[:, lh, cols]
             else:
-                rhs, rhs_scale = b8[:, lh, cols].bitcast(E4M3), b8_plane[:, lh, cols]
+                rhs, rhs_scale = b8[lh][:, cols].bitcast(E4M3), b8_plane[:, lh, cols]
             nc.tensor.matmul_mx(
                 out=y_bank(mt, nh)[:] if bank is None else bank[:, : c1 - c0],
                 lhsT=h_codes[lh, mt].bitcast(E5M2),
@@ -238,9 +236,17 @@ def tile_mix_kfac_mix_res_sgd_kernel(
 
         round_whole(1)
         round_whole(0)
-        for jp in range(2):
-            for q in range(4):
-                drain_h(nc.vector if (jp, q) == (0, 1) else nc.scalar, 0, jp, q)
+        for jp, q in ((0, 0), (0, 1), (0, 2), (0, 3), (1, 0)):
+            drain_h(nc.vector if q % 2 else nc.scalar, 0, jp, q)
+        cast_g(nc.scalar, 1, 1, 0, SHARE_WHOLE, P, 0, 2)
+        for q in range(1, 4):
+            drain_h(nc.scalar, 0, 1, q)
+        cast_g(nc.vector, 1, 1, 0, 0, SHARE_WHOLE, 0, 2)
+        cast_g(nc.vector, 1, 1, 0, 0, FILL, 2, PACK)
+        quantize_g(1, 1, 0, 2)
+        cast_g(nc.vector, 1, 1, 0, FILL, P, 2, PACK)
+        quantize_g(1, 1, 2, PACK)
+        first_product(1, 1)
 
         def round_in_pieces(kh, shared, filler):
             cast_g(nc.vector, kh, 1, 0, 0, CUT, 0, 2)
@@ -253,7 +259,6 @@ def tile_mix_kfac_mix_res_sgd_kernel(
             quantize_g(kh, 1, 2, PACK)
             first_product(kh, 1)
 
-        round_in_pieces(1, 0, FILL)
         cast_g(nc.scalar, 0, 1, 0, 0, SHARE_LAST, 2, PACK)
         interleave_h(nc.scalar, 0, 0)
         round_in_pieces(0, SHARE_LAST, CUT)

@@ -27,8 +27,8 @@ SHARE_WHOLE = 88
 SHARE_LAST = 56
 FILL = 40
 TILES = M // P
-PRM_LOADS = [(0, 3), (3, 5), (5, 8)]
-STORE_ENDS = [3 * N, 5 * N, 6 * N, 6 * N + 512, 7 * N, 7 * N + 512, 7 * N + 768, 8 * N]
+PRM_LOADS = [(0, 2), (2, 5), (5, 8)]
+STORE_ENDS = [2 * N, 4 * N + 512, 5 * N + 512, 6 * N + 512, 7 * N, 7 * N + 512, 7 * N + 768, 8 * N]
 
 
 def tile_mix_kfac_mix_res_sgd_kernel(
@@ -91,9 +91,9 @@ def tile_mix_kfac_mix_res_sgd_kernel(
         load_g(0, 0, 0, P)
         a8 = load_fp8("a8", a8_words[0])
         load_scales(a8_plane, a8_scales)
-        load_g(1, 1, 0, P)
-        load_g(0, 1, 0, CUT)
-        load_g(0, 1, CUT, P)
+        for kh in (1, 0):
+            load_g(kh, 1, 0, CUT)
+            load_g(kh, 1, CUT, P)
         b4 = tile("b4", [P, 2, 2 * N], U8)
         nc.sync.dma_start(out=b4[:].bitcast(I32), in_=b4_words.rearrange("a p w -> p a w").bitcast(I32))
         load_scales(b4_plane, b4_scales)
@@ -236,17 +236,9 @@ def tile_mix_kfac_mix_res_sgd_kernel(
 
         round_whole(1)
         round_whole(0)
-        for jp, q in ((0, 0), (0, 1), (0, 2), (0, 3), (1, 0)):
-            drain_h(nc.vector if q % 2 else nc.scalar, 0, jp, q)
-        cast_g(nc.scalar, 1, 1, 0, SHARE_WHOLE, P, 0, 2)
-        for q in range(1, 4):
-            drain_h(nc.scalar, 0, 1, q)
-        cast_g(nc.vector, 1, 1, 0, 0, SHARE_WHOLE, 0, 2)
-        cast_g(nc.vector, 1, 1, 0, 0, FILL, 2, PACK)
-        quantize_g(1, 1, 0, 2)
-        cast_g(nc.vector, 1, 1, 0, FILL, P, 2, PACK)
-        quantize_g(1, 1, 2, PACK)
-        first_product(1, 1)
+        for jp in range(2):
+            for q in range(4):
+                drain_h(nc.vector if (jp, q) == (0, 1) else nc.scalar, 0, jp, q)
 
         def round_in_pieces(kh, shared, filler):
             cast_g(nc.vector, kh, 1, 0, 0, CUT, 0, 2)
@@ -259,6 +251,7 @@ def tile_mix_kfac_mix_res_sgd_kernel(
             quantize_g(kh, 1, 2, PACK)
             first_product(kh, 1)
 
+        round_in_pieces(1, 0, FILL)
         cast_g(nc.scalar, 0, 1, 0, 0, SHARE_LAST, 2, PACK)
         interleave_h(nc.scalar, 0, 0)
         round_in_pieces(0, SHARE_LAST, CUT)
@@ -276,10 +269,14 @@ def tile_mix_kfac_mix_res_sgd_kernel(
                 interleave_h(nc.vector, *following)
             quantize_h(*now)
 
+        one_stationary = [(0, 0), (0, 1), (1, 1), (1, 0)]
         for tier in range(2):
-            for mt in range(4):
+            for mt in range(2):
                 for nh in range(2):
                     second_product(mt, nh, 0, tier, tier == 0, False)
+        for mt in range(2, 4):
+            for tier, nh in one_stationary:
+                second_product(mt, nh, 0, tier, tier == 0, False)
         for mt in range(4):
             for nh in range(2):
                 for tier in (nh, 1 - nh):

@@ -119,9 +119,11 @@ def tile_mix_kfac_mix_res_sgd_kernel(
                 nc.vector.tensor_copy(out=dst, in_=src)
 
         def cast_g(engine, kh, lh, first, c0, c1, j0=0, j1=PACK):
-            dst = g_bf[kh, lh][:, j0:j1, c0:c1, :].rearrange("p j c t -> p c t j")
+            walk = "p c j t" if engine is nc.scalar else "p c t j"
+            dst = g_bf[kh, lh][:, j0:j1, c0:c1, :].rearrange("p j c t -> " + walk)
             src = g_raw[kh, lh, first][:, :, PACK * (c0 - first) : PACK * (c1 - first)]
-            copy(engine, dst, src.rearrange("p t (c j) -> p c t j", j=PACK)[:, :, :, j0:j1])
+            src = src.rearrange("p t (c j) -> p t c j", j=PACK)[:, :, :, j0:j1]
+            copy(engine, dst, src.rearrange("p t c j -> " + walk))
 
         def quantize_g(kh, lh, j0=0, j1=PACK):
             for j in range(j0, j1):

@@ -27,8 +27,8 @@ SHARE_WHOLE = 88
 SHARE_LAST = 56
 FILL = 40
 TILES = M // P
-PRM_LOADS = [(0, 2), (2, 5), (5, 8)]
-STORE_ENDS = [2 * N, 4 * N + 512, 5 * N + 512, 6 * N + 512, 7 * N, 7 * N + 512, 7 * N + 768, 8 * N]
+PRM_LOADS = [(0, 2), (2, 4), (4, 6), (6, 8)]
+STORE_ENDS = [2 * N, 4 * N, 5 * N, 6 * N, 6 * N + 512, 7 * N, 7 * N + 512, 7 * N + 768, 8 * N]
 
 
 def tile_mix_kfac_mix_res_sgd_kernel(

from contextlib import ExitStack

import concourse.mybir as mybir

K, L, M, N = 1024, 1024, 1024, 1024
FLOPS = 2 * K * L * M + 2 * 2 * L * M * N

F32 = mybir.dt.float32
BF16 = mybir.dt.bfloat16
I32 = mybir.dt.int32
U32 = mybir.dt.uint32
U8 = mybir.dt.uint8
E4M3 = mybir.dt.float8_e4m3fn_x4
E5M2 = mybir.dt.float8_e5m2_x4
E2M1 = mybir.dt.float4_e2m1fn_x4
MULT = mybir.AluOpType.mult
ADD = mybir.AluOpType.add

P = 128
PACK = 4
PASS = P * PACK
BANK = 512
QUARTER = 256
STEP = -0.0625
CUT = 3 * P // 4
SHARE_WHOLE = 88
SHARE_LAST = 56
FILL = 40
TILES = M // P
PRM_LOADS = [(0, 2), (2, 4), (4, 6), (6, 8)]
STORE_ENDS = [2 * N, 4 * N, 5 * N, 6 * N, 6 * N + 512, 7 * N, 7 * N + 512, 7 * N + 768, 8 * N]


def tile_mix_kfac_mix_res_sgd_kernel(
    tc, g, a8_words, a8_scales, a4_words, a4_scales, b4_words, b4_scales, b8_words, b8_scales, prm, out
):
    nc = tc.nc
    with ExitStack() as ctx:
        sb = ctx.enter_context(tc.tile_pool(name="sb", bufs=1))
        psum = ctx.enter_context(tc.psum_pool(name="psum", bufs=1))
        ctx.enter_context(tc.manual_schedule())

        def tile(name, shape, dtype):
            return sb.tile(shape, dtype, name=name, align_bytes=256)

        banks = [psum.tile([P, BANK], F32, name="bank%d" % i) for i in range(8)]

        def shifted(name, width, dtype, skip):
            return tile(name, [P, skip + width], dtype)[:, skip:]

        a_planes = shifted("a_planes", 2 * M, U8, 128).rearrange("p (a n) -> p a n", a=2)
        a4_plane, a8_plane = a_planes[:, 0:1, :], a_planes[:, 1:2, :]
        b4_plane = shifted("b4_plane", 2 * N, U8, 128).rearrange("p (a n) -> p a n", a=2)
        b8_plane = shifted("b8_plane", 2 * N, U8, 128).rearrange("p (a n) -> p a n", a=2)
        for plane in (a4_plane, a8_plane, b4_plane, b8_plane):
            nc.vector.memset(plane.bitcast(I32), 0)

        def load_scales(plane, scales):
            for r in range(4):
                nc.sync.dma_start(
                    out=plane[r:P:32, :, :].bitcast(I32),
                    in_=scales[:, r:16:4, :].rearrange("a q n -> q a n").bitcast(I32),
                )

        g_raw = {}

        def load_g(kh, lh, c0, c1):
            raw = tile("g_raw%d%d_%d" % (kh, lh, c0), [P, PACK, PACK * (c1 - c0)], F32)
            l0 = lh * PASS
            nc.sync.dma_start(
                out=raw[:],
                in_=g[kh * PASS : (kh + 1) * PASS, l0 + PACK * c0 : l0 + PACK * c1].rearrange(
                    "(p t) w -> p t w", t=PACK
                ),
            )
            g_raw[kh, lh, c0] = raw

        def load_fp8(name, words):
            dst = tile(name, [P, N], I32)
            nc.sync.dma_start(out=dst[:], in_=words.rearrange("p n t -> p (n t)").bitcast(I32))
            return dst

        def load_fp4(name, words):
            dst = tile(name, [P, 2 * N], U8)
            nc.sync.dma_start(out=dst[:].bitcast(I32), in_=words.bitcast(I32))
            return dst

        load_g(1, 0, 0, P)
        a4 = load_fp4("a4", a4_words[0])
        load_scales(a4_plane, a4_scales)
        load_g(0, 0, 0, P)
        a8 = load_fp8("a8", a8_words[0])
        load_scales(a8_plane, a8_scales)
        for kh in (1, 0):
            load_g(kh, 1, 0, CUT)
            load_g(kh, 1, CUT, P)
        b4 = tile("b4", [P, 2, 2 * N], U8)
        nc.sync.dma_start(out=b4[:].bitcast(I32), in_=b4_words.rearrange("a p w -> p a w").bitcast(I32))
        load_scales(b4_plane, b4_scales)
        b8 = [load_fp8("b8_0", b8_words[0])]
        load_scales(b8_plane, b8_scales)
        b8.append(load_fp8("b8_1", b8_words[1]))
        prm_rows = prm.rearrange("(p e) n -> p (e n)", e=TILES)
        out_rows = out.rearrange("(p e) n -> p (e n)", e=TILES)
        prm_sb = {}
        for t0, t1 in PRM_LOADS:
            rows = tile("prm%d" % t0, [P, (t1 - t0) * N], F32)
            nc.sync.dma_start(out=rows[:], in_=prm_rows[:, t0 * N : t1 * N])
            for mt in range(t0, t1):
                prm_sb[mt] = rows[:, (mt - t0) * N : (mt - t0 + 1) * N]

        g_bf = {(kh, lh): tile("g_bf%d%d" % (kh, lh), [P, PACK, P, PACK], BF16) for kh in range(2) for lh in range(2)}
        g_codes, g_scale = {}, {}

        def copy(engine, dst, src):
            if engine is nc.scalar:
                nc.scalar.copy(out=dst, in_=src)
            else:
                nc.vector.tensor_copy(out=dst, in_=src)

        def cast_g(engine, kh, lh, first, c0, c1, j0=0, j1=PACK):
            walk = "p c j t" if engine is nc.scalar else "p c t j"
            dst = g_bf[kh, lh][:, j0:j1, c0:c1, :].rearrange("p j c t -> " + walk)
            src = g_raw[kh, lh, first][:, :, PACK * (c0 - first) : PACK * (c1 - first)]
            src = src.rearrange("p t (c j) -> p t c j", j=PACK)[:, :, :, j0:j1]
            copy(engine, dst, src.rearrange("p t c j -> " + walk))

        def quantize_g(kh, lh, j0=0, j1=PACK):
            for j in range(j0, j1):
                codes = shifted("g_codes%d%d%d" % (kh, lh, j), P, I32, 16)
                scale = shifted("g_scale%d%d%d" % (kh, lh, j), P, U8, 192)
                nc.vector.quantize_mx(
                    out=codes[:].bitcast(E5M2),
                    scales=scale[:],
                    in_=g_bf[kh, lh][:, j, :, :].rearrange("p c t -> p (c t)"),
                )
                g_codes[kh, lh, j], g_scale[kh, lh, j] = codes, scale

        def h_bank(jp, q):
            return banks[PACK * jp + q]

        def first_product(kh, lh):
            for jp in range(2):
                for q in range(4):
                    for jj in range(2):
                        cols = slice(q * QUARTER, (q + 1) * QUARTER)
                        if kh == 0:
                            rhs, rhs_scale = a8[:, cols].bitcast(E4M3), a8_plane[:, 0, cols]
                        else:
                            rhs = a4[:, 2 * cols.start : 2 * cols.stop].bitcast(E2M1)
                            rhs_scale = a4_plane[:, 0, cols]
                        nc.tensor.matmul_mx(
                            out=h_bank(jp, q)[:, jj * QUARTER : (jj + 1) * QUARTER],
                            lhsT=g_codes[kh, lh, 2 * jp + jj][:].bitcast(E5M2),
                            lhsT_scale=g_scale[kh, lh, 2 * jp + jj][:],
                            rhs=rhs,
                            rhs_scale=rhs_scale,
                            start=(kh == 1 and jj == 0),
                            stop=(kh == 0 and jj == 1),
                        )

        h_pairs = [tile("h_pairs%d" % lh, [P, 2, 2 * M], BF16) for lh in range(2)]
        h_bf, h_codes, h_scale = {}, {}, {}

        def drain_h(engine, lh, jp, q):
            c = QUARTER // TILES
            copy(
                engine,
                h_pairs[lh][:, jp, :].rearrange("p (e c j) -> p e c j", e=TILES, j=2)[:, :, q * c : (q + 1) * c, :],
                h_bank(jp, q)[:].rearrange("p (j c e) -> p e c j", j=2, e=TILES),
            )

        def interleave_h(engine, lh, q):
            word = U32 if engine is nc.scalar else I32
            dst = tile("h_bf%d%d" % (lh, q), [P, QUARTER * PACK], BF16)
            src = h_pairs[lh][:].bitcast(word)[:, :, q * QUARTER : (q + 1) * QUARTER]
            copy(
                engine,
                dst[:].bitcast(word).rearrange("p (c i j) -> p c j i", i=2, j=2),
                src.rearrange("p j (c i) -> p c j i", i=2),
            )
            h_bf[lh, q] = dst

        def quantize_h(lh, q):
            codes = shifted("h_codes%d%d" % (lh, q), QUARTER, I32, 16)
            scale = shifted("h_scale%d%d" % (lh, q), QUARTER, U8, 192)
            nc.vector.quantize_mx(out=codes[:].bitcast(E5M2), scales=scale[:], in_=h_bf[lh, q][:])
            for e in range(2):
                h_codes[lh, 2 * q + e] = codes[:, e * P : (e + 1) * P]
                h_scale[lh, 2 * q + e] = scale[:, e * P : (e + 1) * P]

        def y_bank(mt, nh):
            return banks[2 * (mt % 4) + nh]

        def second_product(mt, nh, lh, tier, start, stop, c0=0, c1=BANK, bank=None):
            cols = slice(nh * BANK + c0, nh * BANK + c1)
            if tier == 0:
                rhs, rhs_scale = b4[:, lh, 2 * cols.start : 2 * cols.stop].bitcast(E2M1), b4_plane[:, lh, cols]
            else:
                rhs, rhs_scale = b8[lh][:, cols].bitcast(E4M3), b8_plane[:, lh, cols]
            nc.tensor.matmul_mx(
                out=y_bank(mt, nh)[:] if bank is None else bank[:, : c1 - c0],
                lhsT=h_codes[lh, mt].bitcast(E5M2),
                lhsT_scale=h_scale[lh, mt],
                rhs=rhs,
                rhs_scale=rhs_scale,
                start=start,
                stop=stop,
            )

        res = tile("res", [P, TILES * N], F32)
        stored = [0]

        def update(mt, nh, c0=0, c1=BANK, bank=None):
            n0, n1 = nh * BANK + c0, nh * BANK + c1
            nc.vector.scalar_tensor_tensor(
                out=res[:, mt * N + n0 : mt * N + n1],
                in0=y_bank(mt, nh)[:, c0:c1] if bank is None else bank[:, : c1 - c0],
                scalar=STEP,
                in1=prm_sb[mt][:, n0:n1],
                op0=MULT,
                op1=ADD,
            )
            end = mt * N + n1
            if end in STORE_ENDS:
                nc.sync.dma_start(out=out_rows[:, stored[-1] : end], in_=res[:, stored[-1] : end])
                stored.append(end)

        def round_whole(kh):
            for j0 in (0, 2):
                cast_g(nc.scalar, kh, 0, 0, SHARE_WHOLE, P, j0, j0 + 2)
            cast_g(nc.vector, kh, 0, 0, 0, SHARE_WHOLE, 0, 2)
            cast_g(nc.vector, kh, 0, 0, 0, FILL, 2, PACK)
            quantize_g(kh, 0, 0, 2)
            cast_g(nc.vector, kh, 0, 0, FILL, SHARE_WHOLE, 2, PACK)
            quantize_g(kh, 0, 2, PACK)
            first_product(kh, 0)

        round_whole(1)
        round_whole(0)
        for jp in range(2):
            for q in range(4):
                drain_h(nc.vector if (jp, q) == (0, 1) else nc.scalar, 0, jp, q)

        def round_in_pieces(kh, shared, filler):
            cast_g(nc.vector, kh, 1, 0, 0, CUT, 0, 2)
            cast_g(nc.vector, kh, 1, CUT, CUT, P, 0, 2)
            cast_g(nc.vector, kh, 1, 0, shared, filler, 2, PACK)
            quantize_g(kh, 1, 0, 2)
            if filler < CUT:
                cast_g(nc.vector, kh, 1, 0, filler, CUT, 2, PACK)
            cast_g(nc.vector, kh, 1, CUT, CUT, P, 2, PACK)
            quantize_g(kh, 1, 2, PACK)
            first_product(kh, 1)

        round_in_pieces(1, 0, FILL)
        cast_g(nc.scalar, 0, 1, 0, 0, SHARE_LAST, 2, PACK)
        interleave_h(nc.scalar, 0, 0)
        round_in_pieces(0, SHARE_LAST, CUT)
        quantize_h(0, 0)
        interleave_h(nc.vector, 0, 1)
        for jp in range(2):
            for q in range(4):
                drain_h(nc.vector if (jp, q) in ((0, 2), (1, 1)) else nc.scalar, 1, jp, q)
                if (jp, q) == (0, 2):
                    quantize_h(0, 1)
        quarters = [(lh, q) for lh in range(2) for q in range(4)][2:]
        interleave_h(nc.vector, *quarters[0])
        for now, following in zip(quarters, quarters[1:] + [None]):
            if following:
                interleave_h(nc.vector, *following)
            quantize_h(*now)

        one_stationary = [(0, 0), (0, 1), (1, 1), (1, 0)]
        for tier in range(2):
            for mt in range(2):
                for nh in range(2):
                    second_product(mt, nh, 0, tier, tier == 0, False)
        for mt in range(2, 4):
            for tier, nh in one_stationary:
                second_product(mt, nh, 0, tier, tier == 0, False)
        for mt in range(4):
            for nh in range(2):
                for tier in (nh, 1 - nh):
                    second_product(mt, nh, 1, tier, False, tier != nh)
            update(mt, 0)
            update(mt, 1)
        last = M // P - 1
        there = [(0, 0), (0, 1), (1, 1), (1, 0)]
        for mt in range(4, last):
            for nh in range(2):
                for i, (lh, tier) in enumerate(there if nh == 0 else there[::-1]):
                    second_product(mt, nh, lh, tier, i == 0, i == 3)
            update(mt, 0)
            update(mt, 1)
        pieces = [(0, 256, 6), (256, 512, 7), (512, 768, 0), (768, 896, 1), (896, N, 2)]
        for k, (c0, c1, bank) in enumerate(pieces):
            nh = c0 // BANK
            for i, (lh, tier) in enumerate(there if k % 2 == 0 else there[::-1]):
                second_product(last, nh, lh, tier, i == 0, i == 3, c0 - nh * BANK, c1 - nh * BANK, banks[bank])
            update(last, nh, c0 - nh * BANK, c1 - nh * BANK, banks[bank])
